import numpy as np
import ml_dtypes


def mxq(x, axis, fmt="e4m3"):
    dtype, down = {"e4m3": (ml_dtypes.float8_e4m3fn, 7), "e5m2": (ml_dtypes.float8_e5m2, 14)}[fmt]
    v = np.moveaxis(np.asarray(x, np.float32).astype(ml_dtypes.bfloat16).astype(np.float64), axis, -1)
    blocks = v.reshape(v.shape[:-1] + (-1, 32))
    amax = np.abs(blocks).max(-1, keepdims=True)
    byte = np.maximum(np.where(amax > 0, np.frexp(amax)[1] - 1 + 127, 0) - down, 1)
    scale = np.exp2(byte - 127.0)
    codes = (blocks / scale).astype(np.float32).astype(dtype).astype(np.float64)
    return np.moveaxis((codes * scale).reshape(v.shape), -1, axis)


WIDE = False


def mx_kscale(k):
    if not WIDE:
        return np.ones(k)
    levels = np.array([10, -10, 5, -5, 0])
    if k % 512:
        return np.exp2(np.random.permutation(np.resize(levels, k // 32))).repeat(32)
    a = np.empty((k // 512, 16))
    for p in range(k // 512):
        a[p, :8] = np.random.permutation(np.resize(levels, 8))
        for g in range(8):
            far = levels[np.abs(levels - a[p, g]) >= 10]
            a[p, g + 8] = far[np.random.randint(len(far))]
    return np.exp2(a.ravel()).repeat(32)


def f64(x):
    return np.asarray(x).astype(np.float64)


def striped8(idx):
    return np.concatenate([v.reshape(-1, 16).T for v in idx]).astype(np.uint16)


def unstriped8(offs):
    return np.stack([offs[16 * g:16 * g + 16].T.reshape(-1) for g in range(8)]).astype(np.int64)


E2M1 = np.array([0.0, 0.5, 1.0, 1.5, 2.0, 3.0, 4.0, 6.0, -0.0, -0.5, -1.0, -1.5, -2.0, -3.0, -4.0, -6.0])


def pack_weight(w, fmt):
    k, n = w.shape
    w = f64(np.asarray(w, np.float32).astype(ml_dtypes.bfloat16)).reshape(k // 32, 32, n)
    amax = np.abs(w).max(1)
    if fmt == "e4m3":
        byte = np.frexp(amax)[1] - 1 + 127 - 7
    else:
        mant, ex = np.frexp(amax / 6.0)
        byte = np.where(mant > 0.5, ex, ex - 1) + 127
    byte = np.clip(np.where(amax > 0, byte, 1), 1, 254)
    scaled = (w * np.exp2(127.0 - byte)[:, None, :]).reshape(k, n).astype(np.float32)
    by_word = np.ascontiguousarray(scaled.reshape(k // 512, 128, 4, n).transpose(0, 1, 3, 2))
    if fmt == "e4m3":
        words = by_word.astype(ml_dtypes.float8_e4m3fn).view(np.uint8)
    else:
        c = by_word.astype(ml_dtypes.float4_e2m1fn).view(np.uint8) & 0xF
        words = (c[..., 0::2] | (c[..., 1::2] << 4)).reshape(k // 512, 128, 2 * n)
    return np.ascontiguousarray(words), np.ascontiguousarray(byte.astype(np.uint8).reshape(k // 512, 16, n))


def unpack_weight(words, scales, fmt):
    g, _, n = scales.shape
    words = np.ascontiguousarray(words).reshape(g, 128, n, -1)
    if fmt == "e4m3":
        vals = words.view(ml_dtypes.float8_e4m3fn).astype(np.float64)
    else:
        nib = np.empty((g, 128, n, 4), np.uint8)
        nib[..., 0::2] = words & 0xF
        nib[..., 1::2] = words >> 4
        vals = E2M1[nib]
    vals = vals * np.repeat(np.exp2(scales.astype(np.float64) - 127.0), 8, axis=1)[..., None]
    return vals.transpose(0, 1, 3, 2).reshape(g * 512, n)


K, M, T, S = 1024, 256, 1024, 512


def setup_inputs():
    n = np.random.standard_normal
    s = mx_kscale(K)[:, None]
    p_w = pack_weight(n((K, M)) / np.sqrt(K) / s, "e2m1")
    return {
        "xT": (n((K, T)) * s).astype(np.float32),
        "w_words": p_w[0],
        "w_scales": p_w[1],
        "wgt": np.repeat(np.random.uniform(0.5, 2.0, (8, S)), 16, axis=0).astype(np.float32),
        "offs": striped8(np.stack([np.random.permutation(T)[:S] for _ in range(8)])),
    }


def reference(xT, w_words, w_scales, wgt, offs):
    idx = unstriped8(offs)
    group = np.arange(K) % 512 // 64
    xg = f64(wgt)[np.arange(K) // 4 % 128] * f64(xT)[np.arange(K)[:, None], idx[group]]
    xT_ = mxq(xg, 0, "e4m3")
    w_ = unpack_weight(w_words, w_scales, "e2m1")
    y = xT_.T @ w_
    return y

@@ -1,0 +1,136 @@
+from contextlib import ExitStack
+
+import concourse.mybir as mybir
+
+K, N_OUT, T, S = 1024, 256, 1024, 512
+FLOPS = 2 * K * N_OUT * S
+
+F32 = mybir.dt.float32
+BF16 = mybir.dt.bfloat16
+I32 = mybir.dt.int32
+U32 = mybir.dt.uint32
+U16 = mybir.dt.uint16
+U8 = mybir.dt.uint8
+E4M3X4 = mybir.dt.float8_e4m3fn_x4
+E2M1X4 = mybir.dt.float4_e2m1fn_x4
+MULT = mybir.AluOpType.mult
+
+P = 128
+PACK = 4
+K_PASS = P * PACK
+PASSES = K // K_PASS
+HALF = 128
+
+
+def tile_list_heads_tm_none_kernel(tc, xT, w_words, w_scales, wgt, offs, out):
+    nc = tc.nc
+    with ExitStack() as ctx:
+        keep = ctx.enter_context(tc.tile_pool(name="keep", bufs=1))
+        psum = ctx.enter_context(tc.psum_pool(name="psum", bufs=1))
+
+        lists = keep.tile([P, S // 16], U16, name="lists")
+        weight = [keep.tile([P, n], F32, name="wgt%d" % n) for n in (P, S - P)]
+        planes = [[keep.tile([P, T], F32, name="x%d%d" % (a, i)) for i in range(PACK)] for a in range(PASSES)]
+        picked = [keep.tile([P, PACK, S], F32, name="picked%d" % a) for a in range(PASSES)]
+        grouped = [keep.tile([P, S, PACK], BF16, name="grouped%d" % a, align_bytes=64) for a in range(PASSES)]
+        codes = [keep.tile([P, S], U32, name="codes%d" % a, align_bytes=64) for a in range(PASSES)]
+        scales = [keep.tile([P, S], U8, name="scales%d" % a, align_bytes=64) for a in range(PASSES)]
+        w_codes = keep.tile([P, PASSES, 2 * N_OUT], U8, name="w_codes", align_bytes=64)
+        w_sc = keep.tile([P, PASSES, N_OUT], U8, name="w_sc", align_bytes=64)
+        results = [keep.tile([P, N_OUT], F32, name="result%d" % m) for m in range(S // P)]
+        banks = [[psum.tile([P, HALF], F32, name="bank%d%d" % (m, h)) for h in range(2)] for m in range(S // P)]
+        warm = keep.tile([P, 2], F32, name="warm")
+
+        x_view = xT.rearrange("(a p i) t -> a p i t", a=PASSES, i=PACK)
+
+        def load_plane(a, i):
+            nc.sync.dma_start(out=planes[a][i][:], in_=x_view[a, :, i, :])
+
+        nc.gpsimd.memset(w_sc[:].bitcast(I32), 0)
+        nc.gpsimd.memset(warm[:], 0.0)
+        nc.scalar.copy(warm[:, 1:2], warm[:, 0:1])
+        nc.sync.dma_start(lists[:], offs)
+        nc.sync.dma_start(out=weight[0][:], in_=wgt[:, 0:P])
+        load_plane(0, 0)
+        nc.sync.dma_start(out=weight[1][:], in_=wgt[:, P:S])
+        for i in range(1, PACK):
+            load_plane(0, i)
+        for i in range(PACK):
+            load_plane(1, i)
+        for q in range(4):
+            nc.sync.dma_start(
+                out=w_sc[32 * q : 32 * q + 4, :, :].bitcast(I32),
+                in_=w_scales.bitcast(I32)[:, 4 * q : 4 * q + 4, :].rearrange("a q n -> q a n"),
+            )
+        nc.sync.dma_start(out=w_codes[:].bitcast(I32), in_=w_words.bitcast(I32).rearrange("a p n -> p a n"))
+
+
+        def pick(a, i, c0, c1):
+            h, base = (0, 0) if c0 < P else (1, P)
+            nc.vector.tensor_tensor(
+                picked[a][:, i, c0:c1],
+                planes[a][i][:].indirect(lists[:, c0 // 16 : c1 // 16]),
+                weight[h][:, c0 - base : c1 - base],
+                MULT,
+            )
+
+        def interleave(copy, a, c0, c1):
+            copy(
+                grouped[a][:, c0:c1, :].rearrange("p (c n) i -> p c i n", n=4),
+                picked[a][:, :, c0:c1].rearrange("p i (c n) -> p c i n", n=4),
+            )
+
+        def quantise(a, c0, c1):
+            nc.vector.quantize_mx(
+                out=codes[a][:, c0:c1].bitcast(E4M3X4),
+                scales=scales[a][:, c0:c1],
+                in_=grouped[a][:, c0:c1, :].rearrange("p n i -> p (n i)"),
+            )
+
+        def multiply(a, m):
+            cols = slice(P * m, P * (m + 1))
+            for h in range(2):
+                nc.tensor.matmul_mx(
+                    out=banks[m][h][:],
+                    lhsT=codes[a][:, cols].bitcast(E4M3X4),
+                    lhsT_scale=scales[a][:, cols],
+                    rhs=w_codes[:, a, 2 * HALF * h : 2 * HALF * (h + 1)].bitcast(E2M1X4),
+                    rhs_scale=w_sc[:, a, HALF * h : HALF * (h + 1)],
+                    start=(a == 0),
+                    stop=(a == PASSES - 1),
+                )
+
+        def finish(m, copies):
+            for h in range(2):
+                copies[h](results[m][:, HALF * h : HALF * (h + 1)], banks[m][h][:])
+            nc.sync.dma_start(out=out[P * m : P * (m + 1), :], in_=results[m][:])
+
+        S_ = nc.scalar.copy
+        V_ = nc.vector.tensor_copy
+
+        halves = ((0, 256), (256, 512))
+        cuts = ((0, 128), (128, 512))
+        for i in range(PACK):
+            for c0, c1 in cuts:
+                pick(0, i, c0, c1)
+        for c0, c1 in halves:
+            interleave(nc.scalar.copy, 0, c0, c1)
+        for i in (0, 1):
+            for c0, c1 in cuts:
+                pick(1, i, c0, c1)
+        quantise(0, 0, 512)
+        for m in range(4):
+            multiply(0, m)
+        for m in range(4):
+            for i in (2, 3):
+                pick(1, i, 128 * m, 128 * m + 128)
+            if m < 3:
+                interleave(nc.scalar.copy, 1, 128 * m, 128 * m + 128)
+            if m > 0:
+                quantise(1, 128 * (m - 1), 128 * m)
+                multiply(1, m - 1)
+                finish(m - 1, (S_, S_))
+        interleave(nc.vector.tensor_copy, 1, 384, 512)
+        quantise(1, 384, 512)
+        multiply(1, 3)
+        finish(3, (S_, V_))

@@ -27,18 +27,25 @@ def tile_list_heads_tm_none_kernel(tc, xT, w_words, w_scales, wgt, offs, out):
     with ExitStack() as ctx:
         keep = ctx.enter_context(tc.tile_pool(name="keep", bufs=1))
         psum = ctx.enter_context(tc.psum_pool(name="psum", bufs=1))
+        tiles = S // P
+        last = tiles - 1
 
         lists = keep.tile([P, S // 16], U16, name="lists")
-        weight = [keep.tile([P, n], F32, name="wgt%d" % n) for n in (P, S - P)]
+        weight = [
+            keep.tile([P, P], F32, name="weight_first", tag="shared", align_bytes=64),
+            keep.tile([P, S - P], F32, name="weight_rest"),
+        ]
         planes = [[keep.tile([P, T], F32, name="x%d%d" % (a, i)) for i in range(PACK)] for a in range(PASSES)]
-        picked = [keep.tile([P, PACK, S], F32, name="picked%d" % a) for a in range(PASSES)]
+        picked0 = keep.tile([P, PACK, S], F32, name="picked0")
+        picked1 = keep.tile([P, 2, tiles + 2, P], F32, name="picked1")
         grouped = [keep.tile([P, S, PACK], BF16, name="grouped%d" % a, align_bytes=64) for a in range(PASSES)]
         codes = [keep.tile([P, S], U32, name="codes%d" % a, align_bytes=64) for a in range(PASSES)]
-        scales = [keep.tile([P, S], U8, name="scales%d" % a, align_bytes=64) for a in range(PASSES)]
+        scales = {1: keep.tile([P, S], U8, name="scales1", align_bytes=64)}
         w_codes = keep.tile([P, PASSES, 2 * N_OUT], U8, name="w_codes", align_bytes=64)
         w_sc = keep.tile([P, PASSES, N_OUT], U8, name="w_sc", align_bytes=64)
-        results = [keep.tile([P, N_OUT], F32, name="result%d" % m) for m in range(S // P)]
-        banks = [[psum.tile([P, HALF], F32, name="bank%d%d" % (m, h)) for h in range(2)] for m in range(S // P)]
+        results = [keep.tile([P, N_OUT], F32, name="result%d" % m) for m in range(tiles)]
+        whole = [psum.tile([P, N_OUT], F32, name="bank%d" % m) for m in range(last)]
+        parts = [psum.tile([P, HALF], F32, name="part%d" % h) for h in range(2)]
         warm = keep.tile([P, 2], F32, name="warm")
 
         x_view = xT.rearrange("(a p i) t -> a p i t", a=PASSES, i=PACK)
@@ -64,20 +71,21 @@ def tile_list_heads_tm_none_kernel(tc, xT, w_words, w_scales, wgt, offs, out):
             )
         nc.sync.dma_start(out=w_codes[:].bitcast(I32), in_=w_words.bitcast(I32).rearrange("a p n -> p a n"))
 
+        def pick(dst, a, i, c0, c1):
+            factor = weight[0][:, c0:c1] if c0 < P else weight[1][:, c0 - P : c1 - P]
+            nc.vector.tensor_tensor(dst, planes[a][i][:].indirect(lists[:, c0 // 16 : c1 // 16]), factor, MULT)
 
-        def pick(a, i, c0, c1):
-            h, base = (0, 0) if c0 < P else (1, P)
-            nc.vector.tensor_tensor(
-                picked[a][:, i, c0:c1],
-                planes[a][i][:].indirect(lists[:, c0 // 16 : c1 // 16]),
-                weight[h][:, c0 - base : c1 - base],
-                MULT,
+        def interleave0(c0, c1):
+            nc.scalar.copy(
+                grouped[0][:, c0:c1, :].rearrange("p (c n) i -> p c i n", n=4),
+                picked0[:, :, c0:c1].rearrange("p i (c n) -> p c i n", n=4),
             )
 
-        def interleave(copy, a, c0, c1):
+        def interleave1(copy, m, c0, c1):
+            slot = tiles + m % 2
             copy(
-                grouped[a][:, c0:c1, :].rearrange("p (c n) i -> p c i n", n=4),
-                picked[a][:, :, c0:c1].rearrange("p i (c n) -> p c i n", n=4),
+                grouped[1][:, P * m + c0 : P * m + c1, :].rearrange("p (c n) (u v) -> p c u v n", n=4, u=2),
+                picked1[:, :, m : slot + 1 : slot - m, c0:c1].rearrange("p v u (c n) -> p c u v n", n=4),
             )
 
         def quantise(a, c0, c1):
@@ -91,46 +99,58 @@ def tile_list_heads_tm_none_kernel(tc, xT, w_words, w_scales, wgt, offs, out):
             cols = slice(P * m, P * (m + 1))
             for h in range(2):
                 nc.tensor.matmul_mx(
-                    out=banks[m][h][:],
+                    out=parts[h][:] if m == last else whole[m][:, HALF * h : HALF * (h + 1)],
                     lhsT=codes[a][:, cols].bitcast(E4M3X4),
                     lhsT_scale=scales[a][:, cols],
                     rhs=w_codes[:, a, 2 * HALF * h : 2 * HALF * (h + 1)].bitcast(E2M1X4),
                     rhs_scale=w_sc[:, a, HALF * h : HALF * (h + 1)],
-                    start=(a == 0),
-                    stop=(a == PASSES - 1),
+                    start=(a == 0 and (h == 0 or m == last)),
+                    stop=(a == PASSES - 1 and (h == 1 or m == last)),
                 )
 
-        def finish(m, copies):
-            for h in range(2):
-                copies[h](results[m][:, HALF * h : HALF * (h + 1)], banks[m][h][:])
+        def store(m):
             nc.sync.dma_start(out=out[P * m : P * (m + 1), :], in_=results[m][:])
 
-        S_ = nc.scalar.copy
-        V_ = nc.vector.tensor_copy
+        def finish(m):
+            nc.scalar.copy(results[m][:], whole[m][:])
+            store(m)
 
-        halves = ((0, 256), (256, 512))
-        cuts = ((0, 128), (128, 512))
+        def pick_late(m):
+            for v in range(2):
+                pick(picked1[:, v, tiles + m % 2, :], 1, 2 + v, P * m, P * (m + 1))
+
         for i in range(PACK):
-            for c0, c1 in cuts:
-                pick(0, i, c0, c1)
-        for c0, c1 in halves:
-            interleave(nc.scalar.copy, 0, c0, c1)
-        for i in (0, 1):
-            for c0, c1 in cuts:
-                pick(1, i, c0, c1)
-        quantise(0, 0, 512)
-        for m in range(4):
+            pick(picked0[:, i, 0:P], 0, i, 0, P)
+            pick(picked0[:, i, P:S], 0, i, P, S)
+        interleave0(0, S // 2)
+        interleave0(S // 2, S)
+        for v in range(2):
+            pick(picked1[:, v, 0, :], 1, v, 0, P)
+            pick(picked1[:, v, 1:tiles, :].rearrange("p c n -> p (c n)"), 1, v, P, S)
+
+        pick_late(0)
+        interleave1(nc.scalar.copy, 0, 0, P)
+        pick_late(1)
+        interleave1(nc.scalar.copy, 1, 0, P)
+        scales[0] = keep.tile([P, S], U8, name="scales0", tag="shared", align_bytes=64)
+        quantise(0, 0, S)
+        for m in range(tiles):
             multiply(0, m)
-        for m in range(4):
-            for i in (2, 3):
-                pick(1, i, 128 * m, 128 * m + 128)
-            if m < 3:
-                interleave(nc.scalar.copy, 1, 128 * m, 128 * m + 128)
-            if m > 0:
-                quantise(1, 128 * (m - 1), 128 * m)
-                multiply(1, m - 1)
-                finish(m - 1, (S_, S_))
-        interleave(nc.vector.tensor_copy, 1, 384, 512)
-        quantise(1, 384, 512)
+        quantise(1, 0, P)
+        multiply(1, 0)
+        pick_late(2)
+        interleave1(nc.scalar.copy, 2, 0, P)
+        pick_late(3)
+        quantise(1, P, 2 * P)
+        multiply(1, 1)
+        interleave1(nc.scalar.copy, 3, P // 2, P)
+        interleave1(nc.vector.tensor_copy, 3, 0, P // 2)
+        quantise(1, 2 * P, 3 * P)
+        multiply(1, 2)
+        quantise(1, 3 * P, 4 * P)
         multiply(1, 3)
-        finish(3, (S_, V_))
+        for m in range(last):
+            finish(m)
+        nc.scalar.copy(results[last][:, 0:HALF], parts[0][:])
+        nc.vector.tensor_copy(results[last][:, HALF:N_OUT], parts[1][:])
+        store(last)

@@ -31,10 +31,8 @@ def tile_list_heads_tm_none_kernel(tc, xT, w_words, w_scales, wgt, offs, out):
         last = tiles - 1
 
         lists = keep.tile([P, S // 16], U16, name="lists")
-        weight = [
-            keep.tile([P, P], F32, name="weight_first", tag="shared", align_bytes=64),
-            keep.tile([P, S - P], F32, name="weight_rest"),
-        ]
+        weight_first = keep.tile([P, P], F32, name="weight_first", tag="shared", align_bytes=64)
+        weight = keep.tile([P, S], F32, name="weight")
         planes = [[keep.tile([P, T], F32, name="x%d%d" % (a, i)) for i in range(PACK)] for a in range(PASSES)]
         picked0 = keep.tile([P, PACK, S], F32, name="picked0")
         picked1 = keep.tile([P, 2, tiles + 2, P], F32, name="picked1")
@@ -56,10 +54,11 @@ def tile_list_heads_tm_none_kernel(tc, xT, w_words, w_scales, wgt, offs, out):
         nc.gpsimd.memset(w_sc[:].bitcast(I32), 0)
         nc.gpsimd.memset(warm[:], 0.0)
         nc.scalar.copy(warm[:, 1:2], warm[:, 0:1])
-        nc.sync.dma_start(lists[:], offs)
-        nc.sync.dma_start(out=weight[0][:], in_=wgt[:, 0:P])
         load_plane(0, 0)
-        nc.sync.dma_start(out=weight[1][:], in_=wgt[:, P:S])
+        nc.sync.dma_start(lists[:], offs)
+        nc.sync.dma_start(out=weight_first[:], in_=wgt[:, 0:P])
+        nc.sync.dma_start(out=weight[:, P:S], in_=wgt[:, P:S])
+        nc.scalar.copy(weight[:, 0:P], weight_first[:])
         for i in range(1, PACK):
             load_plane(0, i)
         for i in range(PACK):
@@ -72,7 +71,7 @@ def tile_list_heads_tm_none_kernel(tc, xT, w_words, w_scales, wgt, offs, out):
         nc.sync.dma_start(out=w_codes[:].bitcast(I32), in_=w_words.bitcast(I32).rearrange("a p n -> p a n"))
 
         def pick(dst, a, i, c0, c1):
-            factor = weight[0][:, c0:c1] if c0 < P else weight[1][:, c0 - P : c1 - P]
+            factor = weight_first[:] if c1 == P else weight[:, c0:c1]
             nc.vector.tensor_tensor(dst, planes[a][i][:].indirect(lists[:, c0 // 16 : c1 // 16]), factor, MULT)
 
         def interleave0(c0, c1):
@@ -119,14 +118,14 @@ def tile_list_heads_tm_none_kernel(tc, xT, w_words, w_scales, wgt, offs, out):
             for v in range(2):
                 pick(picked1[:, v, tiles + m % 2, :], 1, 2 + v, P * m, P * (m + 1))
 
-        for i in range(PACK):
-            pick(picked0[:, i, 0:P], 0, i, 0, P)
-            pick(picked0[:, i, P:S], 0, i, P, S)
+        pick(picked0[:, 0, 0:P], 0, 0, 0, P)
+        pick(picked0[:, 0, P:S], 0, 0, P, S)
+        for i in range(1, PACK):
+            pick(picked0[:, i, :], 0, i, 0, S)
         interleave0(0, S // 2)
         interleave0(S // 2, S)
         for v in range(2):
-            pick(picked1[:, v, 0, :], 1, v, 0, P)
-            pick(picked1[:, v, 1:tiles, :].rearrange("p c n -> p (c n)"), 1, v, P, S)
+            pick(picked1[:, v, 0:tiles, :].rearrange("p c n -> p (c n)"), 1, v, 0, S)
 
         pick_late(0)
         interleave1(nc.scalar.copy, 0, 0, P)
@@ -143,8 +142,8 @@ def tile_list_heads_tm_none_kernel(tc, xT, w_words, w_scales, wgt, offs, out):
         pick_late(3)
         quantise(1, P, 2 * P)
         multiply(1, 1)
-        interleave1(nc.scalar.copy, 3, P // 2, P)
-        interleave1(nc.vector.tensor_copy, 3, 0, P // 2)
+        interleave1(nc.scalar.copy, 3, 80, P)
+        interleave1(nc.vector.tensor_copy, 3, 0, 80)
         quantise(1, 2 * P, 3 * P)
         multiply(1, 2)
         quantise(1, 3 * P, 4 * P)
@@ -152,5 +151,6 @@ def tile_list_heads_tm_none_kernel(tc, xT, w_words, w_scales, wgt, offs, out):
         for m in range(last):
             finish(m)
         nc.scalar.copy(results[last][:, 0:HALF], parts[0][:])
+        nc.scalar.dma_start(out=out[P * last : S, 0:HALF], in_=results[last][:, 0:HALF])
         nc.vector.tensor_copy(results[last][:, HALF:N_OUT], parts[1][:])
-        store(last)
+        nc.sync.dma_start(out=out[P * last : S, HALF:N_OUT], in_=results[last][:, HALF:N_OUT])

@@ -44,7 +44,6 @@ def tile_list_heads_tm_none_kernel(tc, xT, w_words, w_scales, wgt, offs, out):
         results = [keep.tile([P, N_OUT], F32, name="result%d" % m) for m in range(tiles)]
         whole = [psum.tile([P, N_OUT], F32, name="bank%d" % m) for m in range(last)]
         parts = [psum.tile([P, HALF], F32, name="part%d" % h) for h in range(2)]
-        warm = keep.tile([P, 2], F32, name="warm")
 
         x_view = xT.rearrange("(a p i) t -> a p i t", a=PASSES, i=PACK)
 
@@ -52,8 +51,6 @@ def tile_list_heads_tm_none_kernel(tc, xT, w_words, w_scales, wgt, offs, out):
             nc.sync.dma_start(out=planes[a][i][:], in_=x_view[a, :, i, :])
 
         nc.gpsimd.memset(w_sc[:].bitcast(I32), 0)
-        nc.gpsimd.memset(warm[:], 0.0)
-        nc.scalar.copy(warm[:, 1:2], warm[:, 0:1])
         load_plane(0, 0)
         nc.sync.dma_start(lists[:], offs)
         nc.sync.dma_start(out=weight_first[:], in_=wgt[:, 0:P])

@@ -148,6 +148,5 @@ def tile_list_heads_tm_none_kernel(tc, xT, w_words, w_scales, wgt, offs, out):
         for m in range(last):
             finish(m)
         nc.scalar.copy(results[last][:, 0:HALF], parts[0][:])
-        nc.scalar.dma_start(out=out[P * last : S, 0:HALF], in_=results[last][:, 0:HALF])
         nc.vector.tensor_copy(results[last][:, HALF:N_OUT], parts[1][:])
-        nc.sync.dma_start(out=out[P * last : S, HALF:N_OUT], in_=results[last][:, HALF:N_OUT])
+        store(last)

@@ -20,6 +20,10 @@ PACK = 4
 K_PASS = P * PACK
 PASSES = K // K_PASS
 HALF = 128
+WHOLE = 2
+VECTOR_SHARE = 80
+LATE_AT = (2, 2, 1, 1)
+RING = 3
 
 
 def tile_list_heads_tm_none_kernel(tc, xT, w_words, w_scales, wgt, offs, out):
@@ -28,22 +32,21 @@ def tile_list_heads_tm_none_kernel(tc, xT, w_words, w_scales, wgt, offs, out):
         keep = ctx.enter_context(tc.tile_pool(name="keep", bufs=1))
         psum = ctx.enter_context(tc.psum_pool(name="psum", bufs=1))
         tiles = S // P
-        last = tiles - 1
 
         lists = keep.tile([P, S // 16], U16, name="lists")
-        weight_first = keep.tile([P, P], F32, name="weight_first", tag="shared", align_bytes=64)
-        weight = keep.tile([P, S], F32, name="weight")
         planes = [[keep.tile([P, T], F32, name="x%d%d" % (a, i)) for i in range(PACK)] for a in range(PASSES)]
         picked0 = keep.tile([P, PACK, S], F32, name="picked0")
-        picked1 = keep.tile([P, 2, tiles + 2, P], F32, name="picked1")
-        grouped = [keep.tile([P, S, PACK], BF16, name="grouped%d" % a, align_bytes=64) for a in range(PASSES)]
+        stage = keep.tile([P, 3, 2, tiles, P], F32, name="stage")
+        weight = stage[:, 1, :, :, :].rearrange("p v m n -> p (v m n)")[:, 2 * P : 2 * P + S]
+        grouped0 = keep.tile([P, S, PACK], BF16, name="grouped0", align_bytes=64)
+        ring = keep.tile([P, RING, P, PACK], BF16, name="ring", align_bytes=64)
         codes = [keep.tile([P, S], U32, name="codes%d" % a, align_bytes=64) for a in range(PASSES)]
-        scales = {1: keep.tile([P, S], U8, name="scales1", align_bytes=64)}
+        scales = [keep.tile([P, S], U8, name="scales%d" % a, align_bytes=64) for a in range(PASSES)]
         w_codes = keep.tile([P, PASSES, 2 * N_OUT], U8, name="w_codes", align_bytes=64)
         w_sc = keep.tile([P, PASSES, N_OUT], U8, name="w_sc", align_bytes=64)
         results = [keep.tile([P, N_OUT], F32, name="result%d" % m) for m in range(tiles)]
-        whole = [psum.tile([P, N_OUT], F32, name="bank%d" % m) for m in range(last)]
-        parts = [psum.tile([P, HALF], F32, name="part%d" % h) for h in range(2)]
+        whole = [psum.tile([P, N_OUT], F32, name="bank%d" % m) for m in range(WHOLE)]
+        parts = {m: [psum.tile([P, HALF], F32, name="part%d%d" % (m, h)) for h in range(2)] for m in range(WHOLE, tiles)}
 
         x_view = xT.rearrange("(a p i) t -> a p i t", a=PASSES, i=PACK)
 
@@ -51,11 +54,10 @@ def tile_list_heads_tm_none_kernel(tc, xT, w_words, w_scales, wgt, offs, out):
             nc.sync.dma_start(out=planes[a][i][:], in_=x_view[a, :, i, :])
 
         nc.gpsimd.memset(w_sc[:].bitcast(I32), 0)
-        load_plane(0, 0)
         nc.sync.dma_start(lists[:], offs)
-        nc.sync.dma_start(out=weight_first[:], in_=wgt[:, 0:P])
+        nc.sync.dma_start(out=weight[:, 0:P], in_=wgt[:, 0:P])
+        load_plane(0, 0)
         nc.sync.dma_start(out=weight[:, P:S], in_=wgt[:, P:S])
-        nc.scalar.copy(weight[:, 0:P], weight_first[:])
         for i in range(1, PACK):
             load_plane(0, i)
         for i in range(PACK):
@@ -68,85 +70,85 @@ def tile_list_heads_tm_none_kernel(tc, xT, w_words, w_scales, wgt, offs, out):
         nc.sync.dma_start(out=w_codes[:].bitcast(I32), in_=w_words.bitcast(I32).rearrange("a p n -> p a n"))
 
         def pick(dst, a, i, c0, c1):
-            factor = weight_first[:] if c1 == P else weight[:, c0:c1]
-            nc.vector.tensor_tensor(dst, planes[a][i][:].indirect(lists[:, c0 // 16 : c1 // 16]), factor, MULT)
+            nc.vector.tensor_tensor(dst, planes[a][i][:].indirect(lists[:, c0 // 16 : c1 // 16]), weight[:, c0:c1], MULT)
+
+        def pick_late(v, m):
+            pick(stage[:, LATE_AT[m], v, m, :], 1, 2 + v, P * m, P * (m + 1))
 
         def interleave0(c0, c1):
             nc.scalar.copy(
-                grouped[0][:, c0:c1, :].rearrange("p (c n) i -> p c i n", n=4),
+                grouped0[:, c0:c1, :].rearrange("p (c n) i -> p c i n", n=4),
                 picked0[:, :, c0:c1].rearrange("p i (c n) -> p c i n", n=4),
             )
 
         def interleave1(copy, m, c0, c1):
-            slot = tiles + m % 2
+            u = LATE_AT[m]
             copy(
-                grouped[1][:, P * m + c0 : P * m + c1, :].rearrange("p (c n) (u v) -> p c u v n", n=4, u=2),
-                picked1[:, :, m : slot + 1 : slot - m, c0:c1].rearrange("p v u (c n) -> p c u v n", n=4),
+                ring[:, m % RING, c0:c1, :].rearrange("p (c n) (u v) -> p c u v n", n=4, u=2),
+                stage[:, 0 : u + 1 : u, :, m, c0:c1].rearrange("p u v (c n) -> p c u v n", n=4),
             )
 
-        def quantise(a, c0, c1):
+        def quantise(a, c0, c1, grouped):
             nc.vector.quantize_mx(
                 out=codes[a][:, c0:c1].bitcast(E4M3X4),
                 scales=scales[a][:, c0:c1],
-                in_=grouped[a][:, c0:c1, :].rearrange("p n i -> p (n i)"),
+                in_=grouped.rearrange("p n i -> p (n i)"),
             )
 
         def multiply(a, m):
             cols = slice(P * m, P * (m + 1))
             for h in range(2):
                 nc.tensor.matmul_mx(
-                    out=parts[h][:] if m == last else whole[m][:, HALF * h : HALF * (h + 1)],
+                    out=whole[m][:, HALF * h : HALF * (h + 1)] if m < WHOLE else parts[m][h][:],
                     lhsT=codes[a][:, cols].bitcast(E4M3X4),
                     lhsT_scale=scales[a][:, cols],
                     rhs=w_codes[:, a, 2 * HALF * h : 2 * HALF * (h + 1)].bitcast(E2M1X4),
                     rhs_scale=w_sc[:, a, HALF * h : HALF * (h + 1)],
-                    start=(a == 0 and (h == 0 or m == last)),
-                    stop=(a == PASSES - 1 and (h == 1 or m == last)),
+                    start=(a == 0 and (h == 0 or m >= WHOLE)),
+                    stop=(a == PASSES - 1 and (h == 1 or m >= WHOLE)),
                 )
 
-        def store(m):
+        def finish(m):
+            if m < WHOLE:
+                (nc.scalar.copy, nc.vector.tensor_copy)[m](results[m][:], whole[m][:])
+            else:
+                nc.scalar.copy(results[m][:, 0:HALF], parts[m][0][:])
+                nc.vector.tensor_copy(results[m][:, HALF:N_OUT], parts[m][1][:])
             nc.sync.dma_start(out=out[P * m : P * (m + 1), :], in_=results[m][:])
 
-        def finish(m):
-            nc.scalar.copy(results[m][:], whole[m][:])
-            store(m)
-
-        def pick_late(m):
-            for v in range(2):
-                pick(picked1[:, v, tiles + m % 2, :], 1, 2 + v, P * m, P * (m + 1))
+        def quantise_late(m):
+            quantise(1, P * m, P * (m + 1), ring[:, m % RING, :, :])
+            multiply(1, m)
 
         pick(picked0[:, 0, 0:P], 0, 0, 0, P)
         pick(picked0[:, 0, P:S], 0, 0, P, S)
-        for i in range(1, PACK):
+        for i in range(1, PACK - 1):
             pick(picked0[:, i, :], 0, i, 0, S)
-        interleave0(0, S // 2)
-        interleave0(S // 2, S)
+        for c0 in (0, S // 2):
+            pick(picked0[:, PACK - 1, c0 : c0 + S // 2], 0, PACK - 1, c0, c0 + S // 2)
+            interleave0(c0, c0 + S // 2)
         for v in range(2):
-            pick(picked1[:, v, 0:tiles, :].rearrange("p c n -> p (c n)"), 1, v, 0, S)
-
-        pick_late(0)
-        interleave1(nc.scalar.copy, 0, 0, P)
-        pick_late(1)
-        interleave1(nc.scalar.copy, 1, 0, P)
-        scales[0] = keep.tile([P, S], U8, name="scales0", tag="shared", align_bytes=64)
-        quantise(0, 0, S)
+            pick(stage[:, 0, v, :, :].rearrange("p m n -> p (m n)"), 1, v, 0, S)
+        quantise(0, 0, S, grouped0[:])
         for m in range(tiles):
             multiply(0, m)
-        quantise(1, 0, P)
-        multiply(1, 0)
-        pick_late(2)
+
+        pick_late(0, 0)
+        pick_late(0, 1)
+        pick_late(1, 0)
+        interleave1(nc.scalar.copy, 0, 0, P)
+        pick_late(1, 1)
+        interleave1(nc.scalar.copy, 1, 0, P)
+        pick_late(0, 2)
+        pick_late(1, 2)
         interleave1(nc.scalar.copy, 2, 0, P)
-        pick_late(3)
-        quantise(1, P, 2 * P)
-        multiply(1, 1)
-        interleave1(nc.scalar.copy, 3, 80, P)
-        interleave1(nc.vector.tensor_copy, 3, 0, 80)
-        quantise(1, 2 * P, 3 * P)
-        multiply(1, 2)
-        quantise(1, 3 * P, 4 * P)
-        multiply(1, 3)
-        for m in range(last):
+        pick_late(0, 3)
+        pick_late(1, 3)
+        quantise_late(0)
+        quantise_late(1)
+        interleave1(nc.scalar.copy, 3, VECTOR_SHARE, P)
+        interleave1(nc.vector.tensor_copy, 3, 0, VECTOR_SHARE)
+        quantise_late(2)
+        quantise_late(3)
+        for m in range(tiles):
             finish(m)
-        nc.scalar.copy(results[last][:, 0:HALF], parts[0][:])
-        nc.vector.tensor_copy(results[last][:, HALF:N_OUT], parts[1][:])
-        store(last)

@@ -20,10 +20,9 @@ PACK = 4
 K_PASS = P * PACK
 PASSES = K // K_PASS
 HALF = 128
-WHOLE = 2
+WHOLE = 1
 VECTOR_SHARE = 80
-LATE_AT = (2, 2, 1, 1)
-RING = 3
+LATE_AT = ((4, 5), (6, 7), (0, 8), (1, 4))
 
 
 def tile_list_heads_tm_none_kernel(tc, xT, w_words, w_scales, wgt, offs, out):
@@ -36,10 +35,10 @@ def tile_list_heads_tm_none_kernel(tc, xT, w_words, w_scales, wgt, offs, out):
         lists = keep.tile([P, S // 16], U16, name="lists")
         planes = [[keep.tile([P, T], F32, name="x%d%d" % (a, i)) for i in range(PACK)] for a in range(PASSES)]
         picked0 = keep.tile([P, PACK, S], F32, name="picked0")
-        stage = keep.tile([P, 3, 2, tiles, P], F32, name="stage")
-        weight = stage[:, 1, :, :, :].rearrange("p v m n -> p (v m n)")[:, 2 * P : 2 * P + S]
-        grouped0 = keep.tile([P, S, PACK], BF16, name="grouped0", align_bytes=64)
-        ring = keep.tile([P, RING, P, PACK], BF16, name="ring", align_bytes=64)
+        picked1 = keep.tile([P, 2, S], F32, name="picked1")
+        late = keep.tile([P, 9, P], F32, name="late")
+        weight = late[:, 0:tiles, :].rearrange("p m n -> p (m n)")
+        grouped = [keep.tile([P, S, PACK], BF16, name="grouped%d" % a, align_bytes=64) for a in range(PASSES)]
         codes = [keep.tile([P, S], U32, name="codes%d" % a, align_bytes=64) for a in range(PASSES)]
         scales = [keep.tile([P, S], U8, name="scales%d" % a, align_bytes=64) for a in range(PASSES)]
         w_codes = keep.tile([P, PASSES, 2 * N_OUT], U8, name="w_codes", align_bytes=64)
@@ -73,26 +72,32 @@ def tile_list_heads_tm_none_kernel(tc, xT, w_words, w_scales, wgt, offs, out):
             nc.vector.tensor_tensor(dst, planes[a][i][:].indirect(lists[:, c0 // 16 : c1 // 16]), weight[:, c0:c1], MULT)
 
         def pick_late(v, m):
-            pick(stage[:, LATE_AT[m], v, m, :], 1, 2 + v, P * m, P * (m + 1))
+            pick(late[:, LATE_AT[m][v], :], 1, 2 + v, P * m, P * (m + 1))
 
         def interleave0(c0, c1):
             nc.scalar.copy(
-                grouped0[:, c0:c1, :].rearrange("p (c n) i -> p c i n", n=4),
+                grouped[0][:, c0:c1, :].rearrange("p (c n) i -> p c i n", n=4),
                 picked0[:, :, c0:c1].rearrange("p i (c n) -> p c i n", n=4),
             )
 
-        def interleave1(copy, m, c0, c1):
-            u = LATE_AT[m]
-            copy(
-                ring[:, m % RING, c0:c1, :].rearrange("p (c n) (u v) -> p c u v n", n=4, u=2),
-                stage[:, 0 : u + 1 : u, :, m, c0:c1].rearrange("p u v (c n) -> p c u v n", n=4),
+        def interleave_early(c0, c1):
+            nc.scalar.copy(
+                grouped[1][:, c0:c1, 0:2].rearrange("p (c n) v -> p c v n", n=4),
+                picked1[:, :, c0:c1].rearrange("p v (c n) -> p c v n", n=4),
             )
 
-        def quantise(a, c0, c1, grouped):
+        def interleave1(copy, m, c0, c1):
+            first, second = LATE_AT[m]
+            copy(
+                grouped[1][:, P * m + c0 : P * m + c1, 2:4].rearrange("p (c n) v -> p c v n", n=4),
+                late[:, first : second + 1 : second - first, c0:c1].rearrange("p v (c n) -> p c v n", n=4),
+            )
+
+        def quantise(a, c0, c1):
             nc.vector.quantize_mx(
                 out=codes[a][:, c0:c1].bitcast(E4M3X4),
                 scales=scales[a][:, c0:c1],
-                in_=grouped.rearrange("p n i -> p (n i)"),
+                in_=grouped[a][:, c0:c1, :].rearrange("p n i -> p (n i)"),
             )
 
         def multiply(a, m):
@@ -110,14 +115,14 @@ def tile_list_heads_tm_none_kernel(tc, xT, w_words, w_scales, wgt, offs, out):
 
         def finish(m):
             if m < WHOLE:
-                (nc.scalar.copy, nc.vector.tensor_copy)[m](results[m][:], whole[m][:])
+                nc.scalar.copy(results[m][:], whole[m][:])
             else:
                 nc.scalar.copy(results[m][:, 0:HALF], parts[m][0][:])
                 nc.vector.tensor_copy(results[m][:, HALF:N_OUT], parts[m][1][:])
             nc.sync.dma_start(out=out[P * m : P * (m + 1), :], in_=results[m][:])
 
         def quantise_late(m):
-            quantise(1, P * m, P * (m + 1), ring[:, m % RING, :, :])
+            quantise(1, P * m, P * (m + 1))
             multiply(1, m)
 
         pick(picked0[:, 0, 0:P], 0, 0, 0, P)
@@ -128,8 +133,10 @@ def tile_list_heads_tm_none_kernel(tc, xT, w_words, w_scales, wgt, offs, out):
             pick(picked0[:, PACK - 1, c0 : c0 + S // 2], 0, PACK - 1, c0, c0 + S // 2)
             interleave0(c0, c0 + S // 2)
         for v in range(2):
-            pick(stage[:, 0, v, :, :].rearrange("p m n -> p (m n)"), 1, v, 0, S)
-        quantise(0, 0, S, grouped0[:])
+            pick(picked1[:, v, :], 1, v, 0, S)
+        for c0 in (0, S // 2):
+            interleave_early(c0, c0 + S // 2)
+        quantise(0, 0, S)
         for m in range(tiles):
             multiply(0, m)
 
@@ -143,8 +150,8 @@ def tile_list_heads_tm_none_kernel(tc, xT, w_words, w_scales, wgt, offs, out):
         pick_late(1, 2)
         interleave1(nc.scalar.copy, 2, 0, P)
         pick_late(0, 3)
-        pick_late(1, 3)
         quantise_late(0)
+        pick_late(1, 3)
         quantise_late(1)
         interleave1(nc.scalar.copy, 3, VECTOR_SHARE, P)
         interleave1(nc.vector.tensor_copy, 3, 0, VECTOR_SHARE)

@@ -22,7 +22,7 @@ PASSES = K // K_PASS
 HALF = 128
 WHOLE = 1
 VECTOR_SHARE = 80
-LATE_AT = ((4, 5), (6, 7), (0, 8), (1, 4))
+LATE_AT = ((4, 6), (5, 7), (0, 8), (1, 4))
 
 
 def tile_list_heads_tm_none_kernel(tc, xT, w_words, w_scales, wgt, offs, out):
@@ -53,9 +53,9 @@ def tile_list_heads_tm_none_kernel(tc, xT, w_words, w_scales, wgt, offs, out):
             nc.sync.dma_start(out=planes[a][i][:], in_=x_view[a, :, i, :])
 
         nc.gpsimd.memset(w_sc[:].bitcast(I32), 0)
+        load_plane(0, 0)
         nc.sync.dma_start(lists[:], offs)
         nc.sync.dma_start(out=weight[:, 0:P], in_=wgt[:, 0:P])
-        load_plane(0, 0)
         nc.sync.dma_start(out=weight[:, P:S], in_=wgt[:, P:S])
         for i in range(1, PACK):
             load_plane(0, i)
@@ -71,8 +71,9 @@ def tile_list_heads_tm_none_kernel(tc, xT, w_words, w_scales, wgt, offs, out):
         def pick(dst, a, i, c0, c1):
             nc.vector.tensor_tensor(dst, planes[a][i][:].indirect(lists[:, c0 // 16 : c1 // 16]), weight[:, c0:c1], MULT)
 
-        def pick_late(v, m):
-            pick(late[:, LATE_AT[m][v], :], 1, 2 + v, P * m, P * (m + 1))
+        def pick_late(v, m, count=1):
+            at = LATE_AT[m][v]
+            pick(late[:, at : at + count, :].rearrange("p m n -> p (m n)"), 1, 2 + v, P * m, P * (m + count))
 
         def interleave0(c0, c1):
             nc.scalar.copy(
@@ -127,11 +128,9 @@ def tile_list_heads_tm_none_kernel(tc, xT, w_words, w_scales, wgt, offs, out):
 
         pick(picked0[:, 0, 0:P], 0, 0, 0, P)
         pick(picked0[:, 0, P:S], 0, 0, P, S)
-        for i in range(1, PACK - 1):
+        for i in range(1, PACK):
             pick(picked0[:, i, :], 0, i, 0, S)
-        for c0 in (0, S // 2):
-            pick(picked0[:, PACK - 1, c0 : c0 + S // 2], 0, PACK - 1, c0, c0 + S // 2)
-            interleave0(c0, c0 + S // 2)
+        interleave0(0, S)
         for v in range(2):
             pick(picked1[:, v, :], 1, v, 0, S)
         for c0 in (0, S // 2):
@@ -140,16 +139,14 @@ def tile_list_heads_tm_none_kernel(tc, xT, w_words, w_scales, wgt, offs, out):
         for m in range(tiles):
             multiply(0, m)
 
-        pick_late(0, 0)
-        pick_late(0, 1)
+        pick_late(0, 0, 2)
         pick_late(1, 0)
         interleave1(nc.scalar.copy, 0, 0, P)
         pick_late(1, 1)
         interleave1(nc.scalar.copy, 1, 0, P)
-        pick_late(0, 2)
         pick_late(1, 2)
+        pick_late(0, 2, 2)
         interleave1(nc.scalar.copy, 2, 0, P)
-        pick_late(0, 3)
         quantise_late(0)
         pick_late(1, 3)
         quantise_late(1)

@@ -21,8 +21,7 @@ K_PASS = P * PACK
 PASSES = K // K_PASS
 HALF = 128
 WHOLE = 1
-VECTOR_SHARE = 80
-LATE_AT = ((4, 6), (5, 7), (0, 8), (1, 4))
+VECTOR_SHARE = 88
 
 
 def tile_list_heads_tm_none_kernel(tc, xT, w_words, w_scales, wgt, offs, out):
@@ -35,9 +34,8 @@ def tile_list_heads_tm_none_kernel(tc, xT, w_words, w_scales, wgt, offs, out):
         lists = keep.tile([P, S // 16], U16, name="lists")
         planes = [[keep.tile([P, T], F32, name="x%d%d" % (a, i)) for i in range(PACK)] for a in range(PASSES)]
         picked0 = keep.tile([P, PACK, S], F32, name="picked0")
-        picked1 = keep.tile([P, 2, S], F32, name="picked1")
-        late = keep.tile([P, 9, P], F32, name="late")
-        weight = late[:, 0:tiles, :].rearrange("p m n -> p (m n)")
+        picked1 = keep.tile([P, 2, 10, P], F32, name="picked1")
+        weight = picked1[:, 0, 0:tiles, :].rearrange("p m n -> p (m n)")
         grouped = [keep.tile([P, S, PACK], BF16, name="grouped%d" % a, align_bytes=64) for a in range(PASSES)]
         codes = [keep.tile([P, S], U32, name="codes%d" % a, align_bytes=64) for a in range(PASSES)]
         scales = [keep.tile([P, S], U8, name="scales%d" % a, align_bytes=64) for a in range(PASSES)]
@@ -71,9 +69,8 @@ def tile_list_heads_tm_none_kernel(tc, xT, w_words, w_scales, wgt, offs, out):
         def pick(dst, a, i, c0, c1):
             nc.vector.tensor_tensor(dst, planes[a][i][:].indirect(lists[:, c0 // 16 : c1 // 16]), weight[:, c0:c1], MULT)
 
-        def pick_late(v, m, count=1):
-            at = LATE_AT[m][v]
-            pick(late[:, at : at + count, :].rearrange("p m n -> p (m n)"), 1, 2 + v, P * m, P * (m + count))
+        def pick1(i, row, at, m0, m1):
+            pick(picked1[:, row, at : at + m1 - m0, :].rearrange("p m n -> p (m n)"), 1, i, P * m0, P * m1)
 
         def interleave0(c0, c1):
             nc.scalar.copy(
@@ -81,17 +78,10 @@ def tile_list_heads_tm_none_kernel(tc, xT, w_words, w_scales, wgt, offs, out):
                 picked0[:, :, c0:c1].rearrange("p i (c n) -> p c i n", n=4),
             )
 
-        def interleave_early(c0, c1):
-            nc.scalar.copy(
-                grouped[1][:, c0:c1, 0:2].rearrange("p (c n) v -> p c v n", n=4),
-                picked1[:, :, c0:c1].rearrange("p v (c n) -> p c v n", n=4),
-            )
-
-        def interleave1(copy, m, c0, c1):
-            first, second = LATE_AT[m]
+        def pair(copy, half, two, c0):
             copy(
-                grouped[1][:, P * m + c0 : P * m + c1, 2:4].rearrange("p (c n) v -> p c v n", n=4),
-                late[:, first : second + 1 : second - first, c0:c1].rearrange("p v (c n) -> p c v n", n=4),
+                grouped[1][:, c0 : c0 + two.shape[2], 2 * half : 2 * half + 2].rearrange("p (c n) v -> p c v n", n=4),
+                two.rearrange("p v (c n) -> p c v n", n=4),
             )
 
         def quantise(a, c0, c1):
@@ -132,26 +122,29 @@ def tile_list_heads_tm_none_kernel(tc, xT, w_words, w_scales, wgt, offs, out):
             pick(picked0[:, i, :], 0, i, 0, S)
         interleave0(0, S)
         for v in range(2):
-            pick(picked1[:, v, :], 1, v, 0, S)
-        for c0 in (0, S // 2):
-            interleave_early(c0, c0 + S // 2)
+            pick1(v, v, 4, 0, tiles)
+        pair(nc.scalar.copy, 0, picked1[:, :, 4, :], 0)
+        pair(nc.scalar.copy, 0, picked1[:, :, 6:8, :].rearrange("p v m n -> p v (m n)"), 2 * P)
         quantise(0, 0, S)
         for m in range(tiles):
             multiply(0, m)
 
-        pick_late(0, 0, 2)
-        pick_late(1, 0)
-        interleave1(nc.scalar.copy, 0, 0, P)
-        pick_late(1, 1)
-        interleave1(nc.scalar.copy, 1, 0, P)
-        pick_late(1, 2)
-        pick_late(0, 2, 2)
-        interleave1(nc.scalar.copy, 2, 0, P)
+        pick1(2, 0, 8, 0, 2)
+        pick1(3, 1, 8, 0, 1)
+        pair(nc.scalar.copy, 1, picked1[:, :, 8, :], 0)
+        pick1(3, 1, 9, 1, 2)
+        nc.scalar.copy(
+            grouped[1][:, P : 2 * P, :].rearrange("p (c n) (u v) -> p c u v n", n=4, u=2),
+            picked1[:, :, 5:10:4, :].rearrange("p v u (c n) -> p c u v n", n=4),
+        )
+        pick1(3, 1, 0, 2, 3)
+        pick1(2, 0, 0, 2, 4)
+        pair(nc.scalar.copy, 1, picked1[:, :, 0, :], 2 * P)
         quantise_late(0)
-        pick_late(1, 3)
+        pick1(3, 0, 8, 3, 4)
         quantise_late(1)
-        interleave1(nc.scalar.copy, 3, VECTOR_SHARE, P)
-        interleave1(nc.vector.tensor_copy, 3, 0, VECTOR_SHARE)
+        pair(nc.scalar.copy, 1, picked1[:, 0, 1:9:7, VECTOR_SHARE:P], 3 * P + VECTOR_SHARE)
+        pair(nc.vector.tensor_copy, 1, picked1[:, 0, 1:9:7, 0:VECTOR_SHARE], 3 * P)
         quantise_late(2)
         quantise_late(3)
         for m in range(tiles):

@@ -20,8 +20,7 @@ PACK = 4
 K_PASS = P * PACK
 PASSES = K // K_PASS
 HALF = 128
-WHOLE = 1
-VECTOR_SHARE = 88
+WHOLE = 2
 
 
 def tile_list_heads_tm_none_kernel(tc, xT, w_words, w_scales, wgt, offs, out):
@@ -33,10 +32,14 @@ def tile_list_heads_tm_none_kernel(tc, xT, w_words, w_scales, wgt, offs, out):
 
         lists = keep.tile([P, S // 16], U16, name="lists")
         planes = [[keep.tile([P, T], F32, name="x%d%d" % (a, i)) for i in range(PACK)] for a in range(PASSES)]
-        picked0 = keep.tile([P, PACK, S], F32, name="picked0")
-        picked1 = keep.tile([P, 2, 10, P], F32, name="picked1")
-        weight = picked1[:, 0, 0:tiles, :].rearrange("p m n -> p (m n)")
-        grouped = [keep.tile([P, S, PACK], BF16, name="grouped%d" % a, align_bytes=64) for a in range(PASSES)]
+        stage = keep.tile([P, 32, P], F32, name="stage")
+        weight = stage[:, 0:tiles, :].rearrange("p m n -> p (m n)")
+        grouped0 = keep.tile([P, S, PACK], BF16, name="grouped0", align_bytes=64)
+        late0 = keep.tile([P, P, PACK], BF16, name="late0", align_bytes=64)
+        late1 = keep.tile([P, P, PACK], BF16, name="late1", tag="shared", align_bytes=64)
+        late23 = keep.tile([P, 2 * P, PACK], BF16, name="late23", align_bytes=64)
+        late = [late0[:], late1[:], late23[:, 0:P, :], late23[:, P : 2 * P, :]]
+        held = {}
         codes = [keep.tile([P, S], U32, name="codes%d" % a, align_bytes=64) for a in range(PASSES)]
         scales = [keep.tile([P, S], U8, name="scales%d" % a, align_bytes=64) for a in range(PASSES)]
         w_codes = keep.tile([P, PASSES, 2 * N_OUT], U8, name="w_codes", align_bytes=64)
@@ -69,26 +72,29 @@ def tile_list_heads_tm_none_kernel(tc, xT, w_words, w_scales, wgt, offs, out):
         def pick(dst, a, i, c0, c1):
             nc.vector.tensor_tensor(dst, planes[a][i][:].indirect(lists[:, c0 // 16 : c1 // 16]), weight[:, c0:c1], MULT)
 
-        def pick1(i, row, at, m0, m1):
-            pick(picked1[:, row, at : at + m1 - m0, :].rearrange("p m n -> p (m n)"), 1, i, P * m0, P * m1)
+        def pick_to(a, i, at, m0, m1):
+            pick(stage[:, at : at + m1 - m0, :].rearrange("p m n -> p (m n)"), a, i, P * m0, P * m1)
 
-        def interleave0(c0, c1):
+        def interleave0():
             nc.scalar.copy(
-                grouped[0][:, c0:c1, :].rearrange("p (c n) i -> p c i n", n=4),
-                picked0[:, :, c0:c1].rearrange("p i (c n) -> p c i n", n=4),
+                grouped0[:].rearrange("p (c n) i -> p c i n", n=4),
+                stage[:, 16:32, :].rearrange("p (i m) (c n) -> p (m c) i n", i=PACK, n=4),
             )
 
-        def pair(copy, half, two, c0):
+        def pair(copy, half, two, dst):
             copy(
-                grouped[1][:, c0 : c0 + two.shape[2], 2 * half : 2 * half + 2].rearrange("p (c n) v -> p c v n", n=4),
+                dst[:, :, 2 * half : 2 * half + 2].rearrange("p (c n) v -> p c v n", n=4),
                 two.rearrange("p v (c n) -> p c v n", n=4),
             )
+
+        def scale_of(a, c0, c1):
+            return held[0][:] if (a, c0) == (0, 3 * P) else scales[a][:, c0:c1]
 
         def quantise(a, c0, c1):
             nc.vector.quantize_mx(
                 out=codes[a][:, c0:c1].bitcast(E4M3X4),
-                scales=scales[a][:, c0:c1],
-                in_=grouped[a][:, c0:c1, :].rearrange("p n i -> p (n i)"),
+                scales=scale_of(a, c0, c1),
+                in_=(grouped0[:, c0:c1, :] if a == 0 else late[c0 // P]).rearrange("p n i -> p (n i)"),
             )
 
         def multiply(a, m):
@@ -97,7 +103,7 @@ def tile_list_heads_tm_none_kernel(tc, xT, w_words, w_scales, wgt, offs, out):
                 nc.tensor.matmul_mx(
                     out=whole[m][:, HALF * h : HALF * (h + 1)] if m < WHOLE else parts[m][h][:],
                     lhsT=codes[a][:, cols].bitcast(E4M3X4),
-                    lhsT_scale=scales[a][:, cols],
+                    lhsT_scale=scale_of(a, P * m, P * (m + 1)),
                     rhs=w_codes[:, a, 2 * HALF * h : 2 * HALF * (h + 1)].bitcast(E2M1X4),
                     rhs_scale=w_sc[:, a, HALF * h : HALF * (h + 1)],
                     start=(a == 0 and (h == 0 or m >= WHOLE)),
@@ -116,36 +122,42 @@ def tile_list_heads_tm_none_kernel(tc, xT, w_words, w_scales, wgt, offs, out):
             quantise(1, P * m, P * (m + 1))
             multiply(1, m)
 
-        pick(picked0[:, 0, 0:P], 0, 0, 0, P)
-        pick(picked0[:, 0, P:S], 0, 0, P, S)
+        pick_to(0, 0, 16, 0, 1)
+        pick_to(0, 0, 17, 1, tiles)
         for i in range(1, PACK):
-            pick(picked0[:, i, :], 0, i, 0, S)
-        interleave0(0, S)
+            pick_to(0, i, 16 + tiles * i, 0, tiles)
+        interleave0()
         for v in range(2):
-            pick1(v, v, 4, 0, tiles)
-        pair(nc.scalar.copy, 0, picked1[:, :, 4, :], 0)
-        pair(nc.scalar.copy, 0, picked1[:, :, 6:8, :].rearrange("p v m n -> p v (m n)"), 2 * P)
-        quantise(0, 0, S)
-        for m in range(tiles):
+            pick_to(1, v, 4 + tiles * v, 0, tiles)
+        pair(nc.scalar.copy, 0, stage[:, 4:9:4, :], late[0])
+        pair(nc.scalar.copy, 0, stage[:, 4:12, :].rearrange("p (v m) n -> p v (m n)", v=2)[:, :, 2 * P : S], late23[:])
+        pick_to(1, 2, 12, 0, 2)
+        quantise(0, 0, 2 * P)
+        quantise(0, 2 * P, 3 * P)
+        for m in range(tiles - 1):
             multiply(0, m)
 
-        pick1(2, 0, 8, 0, 2)
-        pick1(3, 1, 8, 0, 1)
-        pair(nc.scalar.copy, 1, picked1[:, :, 8, :], 0)
-        pick1(3, 1, 9, 1, 2)
+        pick_to(1, 3, 16, 0, 1)
+        pair(nc.scalar.copy, 1, stage[:, 12:17:4, :], late[0])
+        pick_to(1, 3, 17, 1, 2)
         nc.scalar.copy(
-            grouped[1][:, P : 2 * P, :].rearrange("p (c n) (u v) -> p c u v n", n=4, u=2),
-            picked1[:, :, 5:10:4, :].rearrange("p v u (c n) -> p c u v n", n=4),
+            late[1].rearrange("p (c n) i -> p c i n", n=4),
+            stage[:, 5:18:4, :].rearrange("p i (c n) -> p c i n", n=4),
         )
-        pick1(3, 1, 0, 2, 3)
-        pick1(2, 0, 0, 2, 4)
-        pair(nc.scalar.copy, 1, picked1[:, :, 0, :], 2 * P)
+        pick_to(1, 2, 18, 2, 3)
+        pick_to(1, 3, 19, 2, 3)
+        pair(nc.scalar.copy, 1, stage[:, 18:20, :], late[2])
         quantise_late(0)
-        pick1(3, 0, 8, 3, 4)
+        finish(0)
+        pick_to(1, 2, 12, 3, 4)
         quantise_late(1)
-        pair(nc.scalar.copy, 1, picked1[:, 0, 1:9:7, VECTOR_SHARE:P], 3 * P + VECTOR_SHARE)
-        pair(nc.vector.tensor_copy, 1, picked1[:, 0, 1:9:7, 0:VECTOR_SHARE], 3 * P)
+        finish(1)
+        pick_to(1, 3, 13, 3, 4)
+        held.update({0: keep.tile([P, P], U8, name="scales03", tag="shared", align_bytes=64)})
+        quantise(0, 3 * P, S)
+        multiply(0, 3)
+        pair(nc.vector.tensor_copy, 1, stage[:, 12:14, :], late[3])
         quantise_late(2)
         quantise_late(3)
-        for m in range(tiles):
+        for m in range(2, tiles):
             finish(m)

@@ -36,9 +36,10 @@ def tile_list_heads_tm_none_kernel(tc, xT, w_words, w_scales, wgt, offs, out):
         weight = stage[:, 0:tiles, :].rearrange("p m n -> p (m n)")
         grouped0 = keep.tile([P, S, PACK], BF16, name="grouped0", align_bytes=64)
         late0 = keep.tile([P, P, PACK], BF16, name="late0", align_bytes=64)
-        late1 = keep.tile([P, P, PACK], BF16, name="late1", tag="shared", align_bytes=64)
-        late23 = keep.tile([P, 2 * P, PACK], BF16, name="late23", align_bytes=64)
-        late = [late0[:], late1[:], late23[:, 0:P, :], late23[:, P : 2 * P, :]]
+        late1 = keep.tile([P, P, PACK], BF16, name="late1", align_bytes=64)
+        late2 = keep.tile([P, P, PACK], BF16, name="late2", tag="shared", align_bytes=64)
+        late3 = keep.tile([P, P, PACK], BF16, name="late3", align_bytes=64)
+        late = [late0[:], late1[:], late2[:], late3[:]]
         held = {}
         codes = [keep.tile([P, S], U32, name="codes%d" % a, align_bytes=64) for a in range(PASSES)]
         scales = [keep.tile([P, S], U8, name="scales%d" % a, align_bytes=64) for a in range(PASSES)]
@@ -130,7 +131,8 @@ def tile_list_heads_tm_none_kernel(tc, xT, w_words, w_scales, wgt, offs, out):
         for v in range(2):
             pick_to(1, v, 4 + tiles * v, 0, tiles)
         pair(nc.scalar.copy, 0, stage[:, 4:9:4, :], late[0])
-        pair(nc.scalar.copy, 0, stage[:, 4:12, :].rearrange("p (v m) n -> p v (m n)", v=2)[:, :, 2 * P : S], late23[:])
+        pair(nc.scalar.copy, 0, stage[:, 6:11:4, :], late[2])
+        pair(nc.scalar.copy, 0, stage[:, 7:12:4, :], late[3])
         pick_to(1, 2, 12, 0, 2)
         quantise(0, 0, 2 * P)
         quantise(0, 2 * P, 3 * P)
@@ -153,11 +155,11 @@ def tile_list_heads_tm_none_kernel(tc, xT, w_words, w_scales, wgt, offs, out):
         quantise_late(1)
         finish(1)
         pick_to(1, 3, 13, 3, 4)
+        quantise_late(2)
+        pair(nc.vector.tensor_copy, 1, stage[:, 12:14, :], late[3])
         held.update({0: keep.tile([P, P], U8, name="scales03", tag="shared", align_bytes=64)})
         quantise(0, 3 * P, S)
         multiply(0, 3)
-        pair(nc.vector.tensor_copy, 1, stage[:, 12:14, :], late[3])
-        quantise_late(2)
         quantise_late(3)
         for m in range(2, tiles):
             finish(m)

@@ -17,10 +17,19 @@ MULT = mybir.AluOpType.mult
 
 P = 128
 PACK = 4
-K_PASS = P * PACK
-PASSES = K // K_PASS
-HALF = 128
-WHOLE = 2
+PASSES = K // (P * PACK)
+TILES = S // P
+LAST = TILES - 1
+HALF = N_OUT // 2
+ONE_BANK = 2
+GROUP = 16
+RUN = 4
+
+WEIGHTS = 0
+EARLY = 4
+THIRD = 12
+PASS0 = 16
+SLOTS = PASS0 + PACK * TILES
 
 
 def tile_list_heads_tm_none_kernel(tc, xT, w_words, w_scales, wgt, offs, out):
@@ -28,26 +37,24 @@ def tile_list_heads_tm_none_kernel(tc, xT, w_words, w_scales, wgt, offs, out):
     with ExitStack() as ctx:
         keep = ctx.enter_context(tc.tile_pool(name="keep", bufs=1))
         psum = ctx.enter_context(tc.psum_pool(name="psum", bufs=1))
-        tiles = S // P
 
-        lists = keep.tile([P, S // 16], U16, name="lists")
+        lists = keep.tile([P, S // GROUP], U16, name="lists")
         planes = [[keep.tile([P, T], F32, name="x%d%d" % (a, i)) for i in range(PACK)] for a in range(PASSES)]
-        stage = keep.tile([P, 32, P], F32, name="stage")
-        weight = stage[:, 0:tiles, :].rearrange("p m n -> p (m n)")
-        grouped0 = keep.tile([P, S, PACK], BF16, name="grouped0", align_bytes=64)
-        late0 = keep.tile([P, P, PACK], BF16, name="late0", align_bytes=64)
-        late1 = keep.tile([P, P, PACK], BF16, name="late1", align_bytes=64)
-        late2 = keep.tile([P, P, PACK], BF16, name="late2", tag="shared", align_bytes=64)
-        late3 = keep.tile([P, P, PACK], BF16, name="late3", align_bytes=64)
-        late = [late0[:], late1[:], late2[:], late3[:]]
-        held = {}
+        stage = keep.tile([P, SLOTS, P], F32, name="stage")
+        weight = stage[:, WEIGHTS : WEIGHTS + TILES, :].rearrange("p m n -> p (m n)")
+        woven0 = keep.tile([P, S, PACK], BF16, name="woven0", align_bytes=64)
+        woven1 = [
+            keep.tile([P, P, PACK], BF16, name="woven1%d" % m, tag="woven1%d" % m, align_bytes=64) for m in range(TILES)
+        ]
         codes = [keep.tile([P, S], U32, name="codes%d" % a, align_bytes=64) for a in range(PASSES)]
         scales = [keep.tile([P, S], U8, name="scales%d" % a, align_bytes=64) for a in range(PASSES)]
         w_codes = keep.tile([P, PASSES, 2 * N_OUT], U8, name="w_codes", align_bytes=64)
         w_sc = keep.tile([P, PASSES, N_OUT], U8, name="w_sc", align_bytes=64)
-        results = [keep.tile([P, N_OUT], F32, name="result%d" % m) for m in range(tiles)]
-        whole = [psum.tile([P, N_OUT], F32, name="bank%d" % m) for m in range(WHOLE)]
-        parts = {m: [psum.tile([P, HALF], F32, name="part%d%d" % (m, h)) for h in range(2)] for m in range(WHOLE, tiles)}
+        results = [keep.tile([P, N_OUT], F32, name="result%d" % m) for m in range(TILES)]
+        banks = [psum.tile([P, N_OUT], F32, name="bank%d" % m) for m in range(ONE_BANK)]
+        halves = {
+            m: [psum.tile([P, HALF], F32, name="half%d%d" % (m, h)) for h in range(2)] for m in range(ONE_BANK, TILES)
+        }
 
         x_view = xT.rearrange("(a p i) t -> a p i t", a=PASSES, i=PACK)
 
@@ -70,96 +77,98 @@ def tile_list_heads_tm_none_kernel(tc, xT, w_words, w_scales, wgt, offs, out):
             )
         nc.sync.dma_start(out=w_codes[:].bitcast(I32), in_=w_words.bitcast(I32).rearrange("a p n -> p a n"))
 
-        def pick(dst, a, i, c0, c1):
-            nc.vector.tensor_tensor(dst, planes[a][i][:].indirect(lists[:, c0 // 16 : c1 // 16]), weight[:, c0:c1], MULT)
-
-        def pick_to(a, i, at, m0, m1):
-            pick(stage[:, at : at + m1 - m0, :].rearrange("p m n -> p (m n)"), a, i, P * m0, P * m1)
-
-        def interleave0():
-            nc.scalar.copy(
-                grouped0[:].rearrange("p (c n) i -> p c i n", n=4),
-                stage[:, 16:32, :].rearrange("p (i m) (c n) -> p (m c) i n", i=PACK, n=4),
+        def pick(a, i, m0, m1, slot):
+            nc.vector.tensor_tensor(
+                stage[:, slot : slot + m1 - m0, :].rearrange("p m n -> p (m n)"),
+                planes[a][i][:].indirect(lists[:, P * m0 // GROUP : P * m1 // GROUP]),
+                weight[:, P * m0 : P * m1],
+                MULT,
             )
 
-        def pair(copy, half, two, dst):
-            copy(
-                dst[:, :, 2 * half : 2 * half + 2].rearrange("p (c n) v -> p c v n", n=4),
-                two.rearrange("p v (c n) -> p c v n", n=4),
-            )
+        def weave(copy, dst, src):
+            copy(dst.rearrange("p (c n) i -> p c i n", n=RUN), src.rearrange("p i (c n) -> p c i n", n=RUN))
 
-        def scale_of(a, c0, c1):
-            return held[0][:] if (a, c0) == (0, 3 * P) else scales[a][:, c0:c1]
+        def slots(first, step, count):
+            return stage[:, first : first + step * (count - 1) + 1 : step, :]
 
-        def quantise(a, c0, c1):
+        def quantise(a, c0, c1, values, scale):
             nc.vector.quantize_mx(
                 out=codes[a][:, c0:c1].bitcast(E4M3X4),
-                scales=scale_of(a, c0, c1),
-                in_=(grouped0[:, c0:c1, :] if a == 0 else late[c0 // P]).rearrange("p n i -> p (n i)"),
+                scales=scale,
+                in_=values.rearrange("p n i -> p (n i)"),
             )
 
-        def multiply(a, m):
-            cols = slice(P * m, P * (m + 1))
+        def multiply(a, m, scale):
             for h in range(2):
                 nc.tensor.matmul_mx(
-                    out=whole[m][:, HALF * h : HALF * (h + 1)] if m < WHOLE else parts[m][h][:],
-                    lhsT=codes[a][:, cols].bitcast(E4M3X4),
-                    lhsT_scale=scale_of(a, P * m, P * (m + 1)),
+                    out=banks[m][:, HALF * h : HALF * (h + 1)] if m < ONE_BANK else halves[m][h][:],
+                    lhsT=codes[a][:, P * m : P * (m + 1)].bitcast(E4M3X4),
+                    lhsT_scale=scale,
                     rhs=w_codes[:, a, 2 * HALF * h : 2 * HALF * (h + 1)].bitcast(E2M1X4),
                     rhs_scale=w_sc[:, a, HALF * h : HALF * (h + 1)],
-                    start=(a == 0 and (h == 0 or m >= WHOLE)),
-                    stop=(a == PASSES - 1 and (h == 1 or m >= WHOLE)),
+                    start=(a == 0 and (h == 0 or m >= ONE_BANK)),
+                    stop=(a == PASSES - 1 and (h == 1 or m >= ONE_BANK)),
                 )
 
-        def finish(m):
-            if m < WHOLE:
-                nc.scalar.copy(results[m][:], whole[m][:])
+        def second_pass(m):
+            scale = scales[1][:, P * m : P * (m + 1)]
+            quantise(1, P * m, P * (m + 1), woven1[m][:], scale)
+            multiply(1, m, scale)
+
+        def store(m):
+            if m < ONE_BANK:
+                nc.scalar.copy(results[m][:], banks[m][:])
             else:
-                nc.scalar.copy(results[m][:, 0:HALF], parts[m][0][:])
-                nc.vector.tensor_copy(results[m][:, HALF:N_OUT], parts[m][1][:])
+                nc.scalar.copy(results[m][:, 0:HALF], halves[m][0][:])
+                nc.vector.tensor_copy(results[m][:, HALF:N_OUT], halves[m][1][:])
             nc.sync.dma_start(out=out[P * m : P * (m + 1), :], in_=results[m][:])
 
-        def quantise_late(m):
-            quantise(1, P * m, P * (m + 1))
-            multiply(1, m)
-
-        pick_to(0, 0, 16, 0, 1)
-        pick_to(0, 0, 17, 1, tiles)
+        pick(0, 0, 0, 1, PASS0)
+        pick(0, 0, 1, TILES, PASS0 + 1)
         for i in range(1, PACK):
-            pick_to(0, i, 16 + tiles * i, 0, tiles)
-        interleave0()
-        for v in range(2):
-            pick_to(1, v, 4 + tiles * v, 0, tiles)
-        pair(nc.scalar.copy, 0, stage[:, 4:9:4, :], late[0])
-        pair(nc.scalar.copy, 0, stage[:, 6:11:4, :], late[2])
-        pair(nc.scalar.copy, 0, stage[:, 7:12:4, :], late[3])
-        pick_to(1, 2, 12, 0, 2)
-        quantise(0, 0, 2 * P)
-        quantise(0, 2 * P, 3 * P)
-        for m in range(tiles - 1):
-            multiply(0, m)
-
-        pick_to(1, 3, 16, 0, 1)
-        pair(nc.scalar.copy, 1, stage[:, 12:17:4, :], late[0])
-        pick_to(1, 3, 17, 1, 2)
+            pick(0, i, 0, TILES, PASS0 + TILES * i)
         nc.scalar.copy(
-            late[1].rearrange("p (c n) i -> p c i n", n=4),
-            stage[:, 5:18:4, :].rearrange("p i (c n) -> p c i n", n=4),
+            woven0[:].rearrange("p (c n) i -> p c i n", n=RUN),
+            stage[:, PASS0:SLOTS, :].rearrange("p (i m) (c n) -> p (m c) i n", i=PACK, n=RUN),
         )
-        pick_to(1, 2, 18, 2, 3)
-        pick_to(1, 3, 19, 2, 3)
-        pair(nc.scalar.copy, 1, stage[:, 18:20, :], late[2])
-        quantise_late(0)
-        finish(0)
-        pick_to(1, 2, 12, 3, 4)
-        quantise_late(1)
-        finish(1)
-        pick_to(1, 3, 13, 3, 4)
-        quantise_late(2)
-        pair(nc.vector.tensor_copy, 1, stage[:, 12:14, :], late[3])
-        held.update({0: keep.tile([P, P], U8, name="scales03", tag="shared", align_bytes=64)})
-        quantise(0, 3 * P, S)
-        multiply(0, 3)
-        quantise_late(3)
-        for m in range(2, tiles):
-            finish(m)
+
+        for i in range(2):
+            pick(1, i, 0, TILES, EARLY + TILES * i)
+        for m in (0, 2, LAST):
+            weave(nc.scalar.copy, woven1[m][:, :, 0:2], slots(EARLY + m, TILES, 2))
+        pick(1, 2, 0, 2, THIRD)
+
+        for m0, m1 in ((0, 2), (2, LAST)):
+            quantise(0, P * m0, P * m1, woven0[:, P * m0 : P * m1, :], scales[0][:, P * m0 : P * m1])
+        for m in range(LAST):
+            multiply(0, m, scales[0][:, P * m : P * (m + 1)])
+
+        pick(1, 3, 0, 1, PASS0)
+        weave(nc.scalar.copy, woven1[0][:, :, 2:4], slots(THIRD, PASS0 - THIRD, 2))
+        pick(1, 3, 1, 2, PASS0 + 1)
+        weave(nc.scalar.copy, woven1[1][:], slots(EARLY + 1, TILES, PACK))
+        pick(1, 2, 2, LAST, PASS0 + 2)
+        pick(1, 3, 2, LAST, PASS0 + 3)
+        weave(nc.scalar.copy, woven1[2][:, :, 2:4], slots(PASS0 + 2, 1, 2))
+
+        second_pass(0)
+        store(0)
+        pick(1, 2, LAST, TILES, THIRD)
+        second_pass(1)
+        store(1)
+        pick(1, 3, LAST, TILES, THIRD + 1)
+
+        second_pass(2)
+        last_scale = keep.tile([P, P], U8, name="last_scale", tag="woven11", align_bytes=64)
+        quantise(0, P * LAST, S, woven0[:, P * LAST : S, :], last_scale[:])
+        multiply(0, LAST, last_scale[:])
+
+        parts = ((0, P // 2), (P // 2, P))
+        for c0, c1 in parts:
+            weave(nc.vector.tensor_copy, woven1[LAST][:, c0:c1, 2:4], stage[:, THIRD : THIRD + 2, c0:c1])
+        for c0, c1 in parts:
+            at = P * LAST
+            quantise(1, at + c0, at + c1, woven1[LAST][:, c0:c1, :], scales[1][:, at + c0 : at + c1])
+        multiply(1, LAST, scales[1][:, P * LAST : S])
+        for m in range(ONE_BANK, TILES):
+            store(m)

@@ -119,8 +119,8 @@ def tile_list_heads_tm_none_kernel(tc, xT, w_words, w_scales, wgt, offs, out):
             if m < ONE_BANK:
                 nc.scalar.copy(results[m][:], banks[m][:])
             else:
-                nc.scalar.copy(results[m][:, 0:HALF], halves[m][0][:])
-                nc.vector.tensor_copy(results[m][:, HALF:N_OUT], halves[m][1][:])
+                nc.vector.tensor_copy(results[m][:, 0:HALF], halves[m][0][:])
+                nc.scalar.copy(results[m][:, HALF:N_OUT], halves[m][1][:])
             nc.sync.dma_start(out=out[P * m : P * (m + 1), :], in_=results[m][:])
 
         pick(0, 0, 0, 1, PASS0)

@@ -23,6 +23,7 @@ LAST = TILES - 1
 HALF = N_OUT // 2
 ONE_BANK = 2
 GROUP = 16
+BLOCK = 32
 RUN = 4
 
 WEIGHTS = 0
@@ -40,7 +41,10 @@ def tile_list_heads_tm_none_kernel(tc, xT, w_words, w_scales, wgt, offs, out):
 
         lists = keep.tile([P, S // GROUP], U16, name="lists")
         planes = [[keep.tile([P, T], F32, name="x%d%d" % (a, i)) for i in range(PACK)] for a in range(PASSES)]
-        stage = keep.tile([P, SLOTS, P], F32, name="stage")
+        stage = keep.tile([P, SLOTS, P], F32, name="stage", align_bytes=64)
+        chunks = keep.tile([P, BLOCK], F32, name="chunks", align_bytes=64)
+        turned = keep.tile([P, BLOCK], F32, name="turned", align_bytes=64)
+        spread = keep.tile([P, S], F32, name="spread", align_bytes=64)
         weight = stage[:, WEIGHTS : WEIGHTS + TILES, :].rearrange("p m n -> p (m n)")
         woven0 = keep.tile([P, S, PACK], BF16, name="woven0", align_bytes=64)
         woven1 = [
@@ -62,10 +66,10 @@ def tile_list_heads_tm_none_kernel(tc, xT, w_words, w_scales, wgt, offs, out):
             nc.sync.dma_start(out=planes[a][i][:], in_=x_view[a, :, i, :])
 
         nc.gpsimd.memset(w_sc[:].bitcast(I32), 0)
+        half_rows = wgt.rearrange("p (h c) -> (p h) c", h=2)[0 : 2 * P : GROUP + 1, :]
+        nc.sync.dma_start(out=chunks[:], in_=half_rows.rearrange("m (s c) -> m s c", c=BLOCK))
         load_plane(0, 0)
         nc.sync.dma_start(lists[:], offs)
-        nc.sync.dma_start(out=weight[:, 0:P], in_=wgt[:, 0:P])
-        nc.sync.dma_start(out=weight[:, P:S], in_=wgt[:, P:S])
         for i in range(1, PACK):
             load_plane(0, i)
         for i in range(PACK):
@@ -123,8 +127,19 @@ def tile_list_heads_tm_none_kernel(tc, xT, w_words, w_scales, wgt, offs, out):
                 nc.scalar.copy(results[m][:, HALF:N_OUT], halves[m][1][:])
             nc.sync.dma_start(out=out[P * m : P * (m + 1), :], in_=results[m][:])
 
-        pick(0, 0, 0, 1, PASS0)
-        pick(0, 0, 1, TILES, PASS0 + 1)
+        nc.vector.transpose(turned[:], chunks[:])
+        by_chunk = turned[:].rearrange("p (h s) -> p s h", h=2)
+        pieces = ((0, P), (P, 2 * P), (2 * P, S))
+        for c0, c1 in pieces:
+            nc.vector.tensor_copy(
+                spread[:, c0:c1].rearrange("p (s h r) -> p s h r", h=2, r=GROUP),
+                by_chunk[:, c0 // BLOCK : c1 // BLOCK, :].unsqueeze(3).to_broadcast([P, (c1 - c0) // BLOCK, 2, GROUP]),
+            )
+        for c0, c1 in pieces:
+            nc.vector.transpose(weight[:, c0:c1], spread[:, c0:c1])
+
+        pick(0, 0, 0, 2, PASS0)
+        pick(0, 0, 2, TILES, PASS0 + 2)
         for i in range(1, PACK):
             pick(0, i, 0, TILES, PASS0 + TILES * i)
         nc.scalar.copy(

@@ -44,7 +44,7 @@ def tile_list_heads_tm_none_kernel(tc, xT, w_words, w_scales, wgt, offs, out):
         stage = keep.tile([P, SLOTS, P], F32, name="stage", align_bytes=64)
         chunks = keep.tile([P, BLOCK], F32, name="chunks", align_bytes=64)
         turned = keep.tile([P, BLOCK], F32, name="turned", align_bytes=64)
-        spread = keep.tile([P, S], F32, name="spread", align_bytes=64)
+        spread = keep.tile([P, LAST * P], F32, name="spread", align_bytes=64)
         weight = stage[:, WEIGHTS : WEIGHTS + TILES, :].rearrange("p m n -> p (m n)")
         woven0 = keep.tile([P, S, PACK], BF16, name="woven0", align_bytes=64)
         woven1 = [
@@ -70,6 +70,7 @@ def tile_list_heads_tm_none_kernel(tc, xT, w_words, w_scales, wgt, offs, out):
         nc.sync.dma_start(out=chunks[:], in_=half_rows.rearrange("m (s c) -> m s c", c=BLOCK))
         load_plane(0, 0)
         nc.sync.dma_start(lists[:], offs)
+        nc.sync.dma_start(out=weight[:, LAST * P : S], in_=wgt[:, LAST * P : S])
         for i in range(1, PACK):
             load_plane(0, i)
         for i in range(PACK):
@@ -129,7 +130,7 @@ def tile_list_heads_tm_none_kernel(tc, xT, w_words, w_scales, wgt, offs, out):
 
         nc.vector.transpose(turned[:], chunks[:])
         by_chunk = turned[:].rearrange("p (h s) -> p s h", h=2)
-        pieces = ((0, P), (P, 2 * P), (2 * P, S))
+        pieces = ((0, P), (P, LAST * P))
         for c0, c1 in pieces:
             nc.vector.tensor_copy(
                 spread[:, c0:c1].rearrange("p (s h r) -> p s h r", h=2, r=GROUP),
@@ -138,8 +139,8 @@ def tile_list_heads_tm_none_kernel(tc, xT, w_words, w_scales, wgt, offs, out):
         for c0, c1 in pieces:
             nc.vector.transpose(weight[:, c0:c1], spread[:, c0:c1])
 
-        pick(0, 0, 0, 2, PASS0)
-        pick(0, 0, 2, TILES, PASS0 + 2)
+        pick(0, 0, 0, 1, PASS0)
+        pick(0, 0, 1, TILES, PASS0 + 1)
         for i in range(1, PACK):
             pick(0, i, 0, TILES, PASS0 + TILES * i)
         nc.scalar.copy(

@@ -156,7 +156,7 @@ def tile_list_heads_tm_none_kernel(tc, xT, w_words, w_scales, wgt, offs, out):
 
         for m0, m1 in ((0, 2), (2, LAST)):
             quantise(0, P * m0, P * m1, woven0[:, P * m0 : P * m1, :], scales[0][:, P * m0 : P * m1])
-        for m in range(LAST):
+        for m in reversed(range(LAST)):
             multiply(0, m, scales[0][:, P * m : P * (m + 1)])
 
         pick(1, 3, 0, 1, PASS0)

@@ -21,7 +21,7 @@ PASSES = K // (P * PACK)
 TILES = S // P
 LAST = TILES - 1
 HALF = N_OUT // 2
-ONE_BANK = 2
+ONE_BANK = 3
 GROUP = 16
 BLOCK = 32
 RUN = 4
@@ -104,15 +104,17 @@ def tile_list_heads_tm_none_kernel(tc, xT, w_words, w_scales, wgt, offs, out):
             )
 
         def multiply(a, m, scale):
-            for h in range(2):
+            sums = [banks[m]] if m < ONE_BANK else halves[m]
+            width = N_OUT // len(sums)
+            for h, acc in enumerate(sums):
                 nc.tensor.matmul_mx(
-                    out=banks[m][:, HALF * h : HALF * (h + 1)] if m < ONE_BANK else halves[m][h][:],
+                    out=acc[:],
                     lhsT=codes[a][:, P * m : P * (m + 1)].bitcast(E4M3X4),
                     lhsT_scale=scale,
-                    rhs=w_codes[:, a, 2 * HALF * h : 2 * HALF * (h + 1)].bitcast(E2M1X4),
-                    rhs_scale=w_sc[:, a, HALF * h : HALF * (h + 1)],
-                    start=(a == 0 and (h == 0 or m >= ONE_BANK)),
-                    stop=(a == PASSES - 1 and (h == 1 or m >= ONE_BANK)),
+                    rhs=w_codes[:, a, 2 * width * h : 2 * width * (h + 1)].bitcast(E2M1X4),
+                    rhs_scale=w_sc[:, a, width * h : width * (h + 1)],
+                    start=(a == 0),
+                    stop=(a == PASSES - 1),
                 )
 
         def second_pass(m):
@@ -154,8 +156,7 @@ def tile_list_heads_tm_none_kernel(tc, xT, w_words, w_scales, wgt, offs, out):
             weave(nc.scalar.copy, woven1[m][:, :, 0:2], slots(EARLY + m, TILES, 2))
         pick(1, 2, 0, 2, THIRD)
 
-        for m0, m1 in ((0, 2), (2, LAST)):
-            quantise(0, P * m0, P * m1, woven0[:, P * m0 : P * m1, :], scales[0][:, P * m0 : P * m1])
+        quantise(0, 0, P * LAST, woven0[:, 0 : P * LAST, :], scales[0][:, 0 : P * LAST])
         for m in reversed(range(LAST)):
             multiply(0, m, scales[0][:, P * m : P * (m + 1)])
 
@@ -163,9 +164,9 @@ def tile_list_heads_tm_none_kernel(tc, xT, w_words, w_scales, wgt, offs, out):
         weave(nc.scalar.copy, woven1[0][:, :, 2:4], slots(THIRD, PASS0 - THIRD, 2))
         pick(1, 3, 1, 2, PASS0 + 1)
         weave(nc.scalar.copy, woven1[1][:], slots(EARLY + 1, TILES, PACK))
-        pick(1, 2, 2, LAST, PASS0 + 2)
-        pick(1, 3, 2, LAST, PASS0 + 3)
-        weave(nc.scalar.copy, woven1[2][:, :, 2:4], slots(PASS0 + 2, 1, 2))
+        pick(1, 2, 2, LAST, WEIGHTS)
+        pick(1, 3, 2, LAST, WEIGHTS + 1)
+        weave(nc.scalar.copy, woven1[2][:, :, 2:4], slots(WEIGHTS, 1, 2))
 
         second_pass(0)
         store(0)
@@ -186,5 +187,5 @@ def tile_list_heads_tm_none_kernel(tc, xT, w_words, w_scales, wgt, offs, out):
             at = P * LAST
             quantise(1, at + c0, at + c1, woven1[LAST][:, c0:c1, :], scales[1][:, at + c0 : at + c1])
         multiply(1, LAST, scales[1][:, P * LAST : S])
-        for m in range(ONE_BANK, TILES):
+        for m in range(2, TILES):
             store(m)

@@ -47,9 +47,9 @@ def tile_list_heads_tm_none_kernel(tc, xT, w_words, w_scales, wgt, offs, out):
         spread = keep.tile([P, LAST * P], F32, name="spread", align_bytes=64)
         weight = stage[:, WEIGHTS : WEIGHTS + TILES, :].rearrange("p m n -> p (m n)")
         woven0 = keep.tile([P, S, PACK], BF16, name="woven0", align_bytes=64)
-        woven1 = [
-            keep.tile([P, P, PACK], BF16, name="woven1%d" % m, tag="woven1%d" % m, align_bytes=64) for m in range(TILES)
-        ]
+        woven_whole = keep.tile([P, P, PACK], BF16, name="woven_whole", tag="woven11", align_bytes=64)
+        woven_pairs = keep.tile([P, LAST * P, PACK], BF16, name="woven_pairs", align_bytes=64)
+        woven1 = [woven_whole] + [woven_pairs[:, P * m : P * (m + 1), :] for m in range(LAST)]
         codes = [keep.tile([P, S], U32, name="codes%d" % a, align_bytes=64) for a in range(PASSES)]
         scales = [keep.tile([P, S], U8, name="scales%d" % a, align_bytes=64) for a in range(PASSES)]
         w_codes = keep.tile([P, PASSES, 2 * N_OUT], U8, name="w_codes", align_bytes=64)
@@ -152,28 +152,28 @@ def tile_list_heads_tm_none_kernel(tc, xT, w_words, w_scales, wgt, offs, out):
 
         for i in range(2):
             pick(1, i, 0, TILES, EARLY + TILES * i)
-        for m in (0, 2, LAST):
-            weave(nc.scalar.copy, woven1[m][:, :, 0:2], slots(EARLY + m, TILES, 2))
+        early = stage[:, EARLY : EARLY + 2 * TILES, :].rearrange("p (i m) n -> p i (m n)", i=2)
+        weave(nc.scalar.copy, woven_pairs[:, :, 0:2], early[:, :, P:S])
         pick(1, 2, 0, 2, THIRD)
 
         quantise(0, 0, P * LAST, woven0[:, 0 : P * LAST, :], scales[0][:, 0 : P * LAST])
-        for m in reversed(range(LAST)):
+        for m in (2, 0, 1):
             multiply(0, m, scales[0][:, P * m : P * (m + 1)])
 
-        pick(1, 3, 0, 1, PASS0)
-        weave(nc.scalar.copy, woven1[0][:, :, 2:4], slots(THIRD, PASS0 - THIRD, 2))
         pick(1, 3, 1, 2, PASS0 + 1)
-        weave(nc.scalar.copy, woven1[1][:], slots(EARLY + 1, TILES, PACK))
-        pick(1, 2, 2, LAST, WEIGHTS)
-        pick(1, 3, 2, LAST, WEIGHTS + 1)
-        weave(nc.scalar.copy, woven1[2][:, :, 2:4], slots(WEIGHTS, 1, 2))
+        weave(nc.scalar.copy, woven1[1][:, :, 2:4], slots(THIRD + 1, PASS0 - THIRD, 2))
+        pick(1, 3, 0, 1, PASS0)
+        weave(nc.scalar.copy, woven1[0][:], slots(EARLY, TILES, PACK))
+        pick(1, 2, 2, LAST, WEIGHTS + 1)
+        pick(1, 3, 2, LAST, WEIGHTS)
+        weave(nc.scalar.copy, woven1[2][:, :, 2:4], stage[:, WEIGHTS : WEIGHTS + 2, :][:, ::-1, :])
 
-        second_pass(0)
-        store(0)
-        pick(1, 2, LAST, TILES, THIRD)
         second_pass(1)
         store(1)
-        pick(1, 3, LAST, TILES, THIRD + 1)
+        pick(1, 2, LAST, TILES, THIRD + 1)
+        second_pass(0)
+        store(0)
+        pick(1, 3, LAST, TILES, PASS0)
 
         second_pass(2)
         last_scale = keep.tile([P, P], U8, name="last_scale", tag="woven11", align_bytes=64)
@@ -182,7 +182,7 @@ def tile_list_heads_tm_none_kernel(tc, xT, w_words, w_scales, wgt, offs, out):
 
         parts = ((0, P // 2), (P // 2, P))
         for c0, c1 in parts:
-            weave(nc.vector.tensor_copy, woven1[LAST][:, c0:c1, 2:4], stage[:, THIRD : THIRD + 2, c0:c1])
+            weave(nc.vector.tensor_copy, woven1[LAST][:, c0:c1, 2:4], slots(THIRD + 1, PASS0 - THIRD - 1, 2)[:, :, c0:c1])
         for c0, c1 in parts:
             at = P * LAST
             quantise(1, at + c0, at + c1, woven1[LAST][:, c0:c1, :], scales[1][:, at + c0 : at + c1])

@@ -23,6 +23,7 @@ LAST = TILES - 1
 HALF = N_OUT // 2
 ONE_BANK = 3
 GROUP = 16
+HELD = 16
 BLOCK = 32
 RUN = 4
 
@@ -145,47 +146,58 @@ def tile_list_heads_tm_none_kernel(tc, xT, w_words, w_scales, wgt, offs, out):
         pick(0, 0, 1, TILES, PASS0 + 1)
         for i in range(1, PACK):
             pick(0, i, 0, TILES, PASS0 + TILES * i)
-        nc.scalar.copy(
-            woven0[:].rearrange("p (c n) i -> p c i n", n=RUN),
-            stage[:, PASS0:SLOTS, :].rearrange("p (i m) (c n) -> p (m c) i n", i=PACK, n=RUN),
-        )
+        staged0 = stage[:, PASS0:SLOTS, :].rearrange("p (i m) n -> p i (m n)", i=PACK)
+
+        def weave0(c0, c1):
+            weave(nc.scalar.copy, woven0[:, c0:c1, :], staged0[:, :, c0:c1])
+
+        weave0(0, 2 * P - HELD)
+        weave0(2 * P, S)
 
         for i in range(2):
             pick(1, i, 0, TILES, EARLY + TILES * i)
         early = stage[:, EARLY : EARLY + 2 * TILES, :].rearrange("p (i m) n -> p i (m n)", i=2)
-        weave(nc.scalar.copy, woven_pairs[:, :, 0:2], early[:, :, P:S])
-        pick(1, 2, 0, 2, THIRD)
+        weave(nc.scalar.copy, woven_pairs[:, 0:P, 0:2], early[:, :, P : 2 * P])
+        weave0(2 * P - HELD, 2 * P)
+        weave(nc.scalar.copy, woven_pairs[:, P : LAST * P, 0:2], early[:, :, 2 * P : S])
+        pick(1, 2, 0, LAST, THIRD)
 
-        quantise(0, 0, P * LAST, woven0[:, 0 : P * LAST, :], scales[0][:, 0 : P * LAST])
-        for m in (2, 0, 1):
-            multiply(0, m, scales[0][:, P * m : P * (m + 1)])
+        def first_pass(m0, m1):
+            quantise(0, P * m0, P * m1, woven0[:, P * m0 : P * m1, :], scales[0][:, P * m0 : P * m1])
+            for m in range(m0, m1):
+                multiply(0, m, scales[0][:, P * m : P * (m + 1)])
 
-        pick(1, 3, 1, 2, PASS0 + 1)
-        weave(nc.scalar.copy, woven1[1][:, :, 2:4], slots(THIRD + 1, PASS0 - THIRD, 2))
-        pick(1, 3, 0, 1, PASS0)
-        weave(nc.scalar.copy, woven1[0][:], slots(EARLY, TILES, PACK))
-        pick(1, 2, 2, LAST, WEIGHTS + 1)
-        pick(1, 3, 2, LAST, WEIGHTS)
-        weave(nc.scalar.copy, woven1[2][:, :, 2:4], stage[:, WEIGHTS : WEIGHTS + 2, :][:, ::-1, :])
+        def late(m):
+            pick(1, 3, m, m + 1, PASS0 + m)
+            if m == 0:
+                weave(nc.scalar.copy, woven1[m][:], slots(EARLY, TILES, PACK))
+            else:
+                weave(nc.scalar.copy, woven1[m][:, :, 2:4], slots(THIRD + m, PASS0 - THIRD, 2))
 
-        second_pass(1)
-        store(1)
-        pick(1, 2, LAST, TILES, THIRD + 1)
+        first_pass(2, 3)
+        late(2)
+        late(0)
+        first_pass(0, 2)
+        late(1)
+
+        second_pass(2)
+        store(2)
+        pick(1, 2, LAST, TILES, THIRD + 2)
         second_pass(0)
         store(0)
         pick(1, 3, LAST, TILES, PASS0)
 
-        second_pass(2)
+        second_pass(1)
         last_scale = keep.tile([P, P], U8, name="last_scale", tag="woven11", align_bytes=64)
         quantise(0, P * LAST, S, woven0[:, P * LAST : S, :], last_scale[:])
         multiply(0, LAST, last_scale[:])
 
         parts = ((0, P // 2), (P // 2, P))
         for c0, c1 in parts:
-            weave(nc.vector.tensor_copy, woven1[LAST][:, c0:c1, 2:4], slots(THIRD + 1, PASS0 - THIRD - 1, 2)[:, :, c0:c1])
+            weave(nc.vector.tensor_copy, woven1[LAST][:, c0:c1, 2:4], slots(THIRD + 2, PASS0 - THIRD - 2, 2)[:, :, c0:c1])
         for c0, c1 in parts:
             at = P * LAST
             quantise(1, at + c0, at + c1, woven1[LAST][:, c0:c1, :], scales[1][:, at + c0 : at + c1])
         multiply(1, LAST, scales[1][:, P * LAST : S])
-        for m in range(2, TILES):
+        for m in (1, LAST):
             store(m)

@@ -175,6 +175,17 @@ def tile_list_heads_tm_none_kernel(tc, xT, w_words, w_scales, wgt, offs, out):
                 weave(nc.scalar.copy, woven1[m][:, :, 2:4], slots(THIRD + m, PASS0 - THIRD, 2))
 
         first_pass(2, 3)
+        idle_bank = psum.tile([P, N_OUT], F32, name="idle_bank")
+        for c0, width in ((0, HALF), (HALF, HALF // 2)):
+            nc.tensor.matmul_mx(
+                out=idle_bank[:, c0 : c0 + width],
+                lhsT=codes[0][:, 2 * P : 3 * P].bitcast(E4M3X4),
+                lhsT_scale=scales[0][:, 2 * P : 3 * P],
+                rhs=w_codes[:, 0, 0 : 2 * width].bitcast(E2M1X4),
+                rhs_scale=w_sc[:, 0, 0:width],
+                start=True,
+                stop=True,
+            )
         late(2)
         late(0)
         first_pass(0, 2)

@@ -24,6 +24,7 @@ HALF = N_OUT // 2
 ONE_BANK = 3
 GROUP = 16
 HELD = 16
+TURNED = 448
 BLOCK = 32
 RUN = 4
 
@@ -45,7 +46,7 @@ def tile_list_heads_tm_none_kernel(tc, xT, w_words, w_scales, wgt, offs, out):
         stage = keep.tile([P, SLOTS, P], F32, name="stage", align_bytes=64)
         chunks = keep.tile([P, BLOCK], F32, name="chunks", align_bytes=64)
         turned = keep.tile([P, BLOCK], F32, name="turned", align_bytes=64)
-        spread = keep.tile([P, LAST * P], F32, name="spread", align_bytes=64)
+        spread = keep.tile([P, TURNED], F32, name="spread", align_bytes=64)
         weight = stage[:, WEIGHTS : WEIGHTS + TILES, :].rearrange("p m n -> p (m n)")
         woven0 = keep.tile([P, S, PACK], BF16, name="woven0", align_bytes=64)
         woven_whole = keep.tile([P, P, PACK], BF16, name="woven_whole", tag="woven11", align_bytes=64)
@@ -71,7 +72,7 @@ def tile_list_heads_tm_none_kernel(tc, xT, w_words, w_scales, wgt, offs, out):
         nc.sync.dma_start(out=chunks[:], in_=half_rows.rearrange("m (s c) -> m s c", c=BLOCK))
         load_plane(0, 0)
         nc.sync.dma_start(lists[:], offs)
-        nc.sync.dma_start(out=weight[:, LAST * P : S], in_=wgt[:, LAST * P : S])
+        nc.sync.dma_start(out=weight[:, TURNED:S], in_=wgt[:, TURNED:S])
         for i in range(1, PACK):
             load_plane(0, i)
         for i in range(PACK):
@@ -133,13 +134,12 @@ def tile_list_heads_tm_none_kernel(tc, xT, w_words, w_scales, wgt, offs, out):
 
         nc.vector.transpose(turned[:], chunks[:])
         by_chunk = turned[:].rearrange("p (h s) -> p s h", h=2)
-        pieces = ((0, P), (P, LAST * P))
-        for c0, c1 in pieces:
+        for c0, c1 in ((0, P), (P, TURNED)):
             nc.vector.tensor_copy(
                 spread[:, c0:c1].rearrange("p (s h r) -> p s h r", h=2, r=GROUP),
                 by_chunk[:, c0 // BLOCK : c1 // BLOCK, :].unsqueeze(3).to_broadcast([P, (c1 - c0) // BLOCK, 2, GROUP]),
             )
-        for c0, c1 in pieces:
+        for c0, c1 in ((0, P), (P, LAST * P), (LAST * P, LAST * P + BLOCK), (LAST * P + BLOCK, TURNED)):
             nc.vector.transpose(weight[:, c0:c1], spread[:, c0:c1])
 
         pick(0, 0, 0, 1, PASS0)

@@ -41,10 +41,10 @@ def tile_list_heads_tm_none_kernel(tc, xT, w_words, w_scales, wgt, offs, out):
         keep = ctx.enter_context(tc.tile_pool(name="keep", bufs=1))
         psum = ctx.enter_context(tc.psum_pool(name="psum", bufs=1))
 
-        lists = keep.tile([P, S // GROUP], U16, name="lists")
-        planes = [[keep.tile([P, T], F32, name="x%d%d" % (a, i)) for i in range(PACK)] for a in range(PASSES)]
-        stage = keep.tile([P, SLOTS, P], F32, name="stage", align_bytes=64)
-        chunks = keep.tile([P, BLOCK], F32, name="chunks", align_bytes=64)
+        lists = keep.tile([P, S // GROUP], U16, name="lists", align_bytes=256)
+        planes = [[keep.tile([P, T], F32, name="x%d%d" % (a, i), align_bytes=256) for i in range(PACK)] for a in range(PASSES)]
+        stage = keep.tile([P, SLOTS, P], F32, name="stage", align_bytes=256)
+        chunks = keep.tile([P, BLOCK], F32, name="chunks", align_bytes=256)
         turned = keep.tile([P, BLOCK], F32, name="turned", align_bytes=64)
         spread = keep.tile([P, TURNED], F32, name="spread", align_bytes=64)
         weight = stage[:, WEIGHTS : WEIGHTS + TILES, :].rearrange("p m n -> p (m n)")
@@ -54,9 +54,9 @@ def tile_list_heads_tm_none_kernel(tc, xT, w_words, w_scales, wgt, offs, out):
         woven1 = [woven_whole] + [woven_pairs[:, P * m : P * (m + 1), :] for m in range(LAST)]
         codes = [keep.tile([P, S], U32, name="codes%d" % a, align_bytes=64) for a in range(PASSES)]
         scales = [keep.tile([P, S], U8, name="scales%d" % a, align_bytes=64) for a in range(PASSES)]
-        w_codes = keep.tile([P, PASSES, 2 * N_OUT], U8, name="w_codes", align_bytes=64)
-        w_sc = keep.tile([P, PASSES, N_OUT], U8, name="w_sc", align_bytes=64)
-        results = [keep.tile([P, N_OUT], F32, name="result%d" % m) for m in range(TILES)]
+        w_codes = keep.tile([P, PASSES, 2 * N_OUT], U8, name="w_codes", align_bytes=256)
+        w_sc = keep.tile([P, PASSES, N_OUT], U8, name="w_sc", align_bytes=256)
+        results = [keep.tile([P, N_OUT], F32, name="result%d" % m, align_bytes=256) for m in range(TILES)]
         banks = [psum.tile([P, N_OUT], F32, name="bank%d" % m) for m in range(ONE_BANK)]
         halves = {
             m: [psum.tile([P, HALF], F32, name="half%d%d" % (m, h)) for h in range(2)] for m in range(ONE_BANK, TILES)

@@ -26,7 +26,7 @@ GROUP = 16
 HELD = 16
 TURNED = 448
 BLOCK = 32
-RUN = 4
+RUN = 2
 
 WEIGHTS = 0
 EARLY = 4

@@ -42,14 +42,14 @@ def tile_list_heads_tm_none_kernel(tc, xT, w_words, w_scales, wgt, offs, out):
         psum = ctx.enter_context(tc.psum_pool(name="psum", bufs=1))
 
         lists = keep.tile([P, S // GROUP], U16, name="lists", align_bytes=256)
-        planes = [[keep.tile([P, T], F32, name="x%d%d" % (a, i), align_bytes=256) for i in range(PACK)] for a in range(PASSES)]
+        planes = [[keep.tile([P, T], F32, name="x%d%d" % (a, i), tag="x%d%d" % (a, i), align_bytes=256) for i in range(PACK)] for a in range(PASSES)]
         stage = keep.tile([P, SLOTS, P], F32, name="stage", align_bytes=256)
         chunks = keep.tile([P, BLOCK], F32, name="chunks", align_bytes=256)
         turned = keep.tile([P, BLOCK], F32, name="turned", align_bytes=64)
         spread = keep.tile([P, TURNED], F32, name="spread", align_bytes=64)
         weight = stage[:, WEIGHTS : WEIGHTS + TILES, :].rearrange("p m n -> p (m n)")
         woven0 = keep.tile([P, S, PACK], BF16, name="woven0", align_bytes=64)
-        woven_whole = keep.tile([P, P, PACK], BF16, name="woven_whole", tag="woven11", align_bytes=64)
+        woven_whole = keep.tile([P, P, PACK], BF16, name="woven_whole", align_bytes=64)
         woven_pairs = keep.tile([P, LAST * P, PACK], BF16, name="woven_pairs", align_bytes=64)
         woven1 = [woven_whole] + [woven_pairs[:, P * m : P * (m + 1), :] for m in range(LAST)]
         codes = [keep.tile([P, S], U32, name="codes%d" % a, align_bytes=64) for a in range(PASSES)]
@@ -199,13 +199,13 @@ def tile_list_heads_tm_none_kernel(tc, xT, w_words, w_scales, wgt, offs, out):
         pick(1, 3, LAST, TILES, PASS0)
 
         second_pass(1)
-        last_scale = keep.tile([P, P], U8, name="last_scale", tag="woven11", align_bytes=64)
-        quantise(0, P * LAST, S, woven0[:, P * LAST : S, :], last_scale[:])
-        multiply(0, LAST, last_scale[:])
 
         parts = ((0, P // 2), (P // 2, P))
         for c0, c1 in parts:
             weave(nc.vector.tensor_copy, woven1[LAST][:, c0:c1, 2:4], slots(THIRD + 2, PASS0 - THIRD - 2, 2)[:, :, c0:c1])
+        last_scale = keep.tile([P, P], U8, name="last_scale", tag="x13", align_bytes=256)
+        quantise(0, P * LAST, S, woven0[:, P * LAST : S, :], last_scale[:])
+        multiply(0, LAST, last_scale[:])
         for c0, c1 in parts:
             at = P * LAST
             quantise(1, at + c0, at + c1, woven1[LAST][:, c0:c1, :], scales[1][:, at + c0 : at + c1])

@@ -162,6 +162,8 @@ def tile_list_heads_tm_none_kernel(tc, xT, w_words, w_scales, wgt, offs, out):
         weave(nc.scalar.copy, woven_pairs[:, P : LAST * P, 0:2], early[:, :, 2 * P : S])
         pick(1, 2, 0, LAST, THIRD)
 
+        parts = ((0, P // 2), (P // 2, P))
+
         def first_pass(m0, m1):
             quantise(0, P * m0, P * m1, woven0[:, P * m0 : P * m1, :], scales[0][:, P * m0 : P * m1])
             for m in range(m0, m1):
@@ -170,7 +172,8 @@ def tile_list_heads_tm_none_kernel(tc, xT, w_words, w_scales, wgt, offs, out):
         def late(m):
             pick(1, 3, m, m + 1, PASS0 + m)
             if m == 0:
-                weave(nc.scalar.copy, woven1[m][:], slots(EARLY, TILES, PACK))
+                for c0, c1 in parts:
+                    weave(nc.scalar.copy, woven1[m][:, c0:c1, :], slots(EARLY, TILES, PACK)[:, :, c0:c1])
             else:
                 weave(nc.scalar.copy, woven1[m][:, :, 2:4], slots(THIRD + m, PASS0 - THIRD, 2))
 
@@ -194,13 +197,14 @@ def tile_list_heads_tm_none_kernel(tc, xT, w_words, w_scales, wgt, offs, out):
         second_pass(2)
         store(2)
         pick(1, 2, LAST, TILES, THIRD + 2)
-        second_pass(0)
+        for c0, c1 in parts:
+            quantise(1, c0, c1, woven1[0][:, c0:c1, :], scales[1][:, c0:c1])
+        multiply(1, 0, scales[1][:, 0:P])
         store(0)
         pick(1, 3, LAST, TILES, PASS0)
 
         second_pass(1)
 
-        parts = ((0, P // 2), (P // 2, P))
         for c0, c1 in parts:
             weave(nc.vector.tensor_copy, woven1[LAST][:, c0:c1, 2:4], slots(THIRD + 2, PASS0 - THIRD - 2, 2)[:, :, c0:c1])
         last_scale = keep.tile([P, P], U8, name="last_scale", tag="x13", align_bytes=256)

@@ -178,17 +178,6 @@ def tile_list_heads_tm_none_kernel(tc, xT, w_words, w_scales, wgt, offs, out):
                 weave(nc.scalar.copy, woven1[m][:, :, 2:4], slots(THIRD + m, PASS0 - THIRD, 2))
 
         first_pass(2, 3)
-        idle_bank = psum.tile([P, N_OUT], F32, name="idle_bank")
-        for c0, width in ((0, HALF), (HALF, HALF // 2)):
-            nc.tensor.matmul_mx(
-                out=idle_bank[:, c0 : c0 + width],
-                lhsT=codes[0][:, 2 * P : 3 * P].bitcast(E4M3X4),
-                lhsT_scale=scales[0][:, 2 * P : 3 * P],
-                rhs=w_codes[:, 0, 0 : 2 * width].bitcast(E2M1X4),
-                rhs_scale=w_sc[:, 0, 0:width],
-                start=True,
-                stop=True,
-            )
         late(2)
         late(0)
         first_pass(0, 2)

from contextlib import ExitStack

import concourse.mybir as mybir

K, N_OUT, T, S = 1024, 256, 1024, 512
FLOPS = 2 * K * N_OUT * S

F32 = mybir.dt.float32
BF16 = mybir.dt.bfloat16
I32 = mybir.dt.int32
U32 = mybir.dt.uint32
U16 = mybir.dt.uint16
U8 = mybir.dt.uint8
E4M3X4 = mybir.dt.float8_e4m3fn_x4
E2M1X4 = mybir.dt.float4_e2m1fn_x4
MULT = mybir.AluOpType.mult

P = 128
PACK = 4
PASSES = K // (P * PACK)
TILES = S // P
LAST = TILES - 1
HALF = N_OUT // 2
ONE_BANK = 3
GROUP = 16
HELD = 16
TURNED = 448
BLOCK = 32
RUN = 2

WEIGHTS = 0
EARLY = 4
THIRD = 12
PASS0 = 16
SLOTS = PASS0 + PACK * TILES


def tile_list_heads_tm_none_kernel(tc, xT, w_words, w_scales, wgt, offs, out):
    nc = tc.nc
    with ExitStack() as ctx:
        keep = ctx.enter_context(tc.tile_pool(name="keep", bufs=1))
        psum = ctx.enter_context(tc.psum_pool(name="psum", bufs=1))

        lists = keep.tile([P, S // GROUP], U16, name="lists", align_bytes=256)
        planes = [[keep.tile([P, T], F32, name="x%d%d" % (a, i), tag="x%d%d" % (a, i), align_bytes=256) for i in range(PACK)] for a in range(PASSES)]
        stage = keep.tile([P, SLOTS, P], F32, name="stage", align_bytes=256)
        chunks = keep.tile([P, BLOCK], F32, name="chunks", align_bytes=256)
        turned = keep.tile([P, BLOCK], F32, name="turned", align_bytes=64)
        spread = keep.tile([P, TURNED], F32, name="spread", align_bytes=64)
        weight = stage[:, WEIGHTS : WEIGHTS + TILES, :].rearrange("p m n -> p (m n)")
        woven0 = keep.tile([P, S, PACK], BF16, name="woven0", align_bytes=64)
        woven_whole = keep.tile([P, P, PACK], BF16, name="woven_whole", align_bytes=64)
        woven_pairs = keep.tile([P, LAST * P, PACK], BF16, name="woven_pairs", align_bytes=64)
        woven1 = [woven_whole] + [woven_pairs[:, P * m : P * (m + 1), :] for m in range(LAST)]
        codes = [keep.tile([P, S], U32, name="codes%d" % a, align_bytes=64) for a in range(PASSES)]
        scales = [keep.tile([P, S], U8, name="scales%d" % a, align_bytes=64) for a in range(PASSES)]
        w_codes = keep.tile([P, PASSES, 2 * N_OUT], U8, name="w_codes", align_bytes=256)
        w_sc = keep.tile([P, PASSES, N_OUT], U8, name="w_sc", align_bytes=256)
        results = [keep.tile([P, N_OUT], F32, name="result%d" % m, align_bytes=256) for m in range(TILES)]
        banks = [psum.tile([P, N_OUT], F32, name="bank%d" % m) for m in range(ONE_BANK)]
        halves = {
            m: [psum.tile([P, HALF], F32, name="half%d%d" % (m, h)) for h in range(2)] for m in range(ONE_BANK, TILES)
        }

        x_view = xT.rearrange("(a p i) t -> a p i t", a=PASSES, i=PACK)

        def load_plane(a, i):
            nc.sync.dma_start(out=planes[a][i][:], in_=x_view[a, :, i, :])

        nc.gpsimd.memset(w_sc[:].bitcast(I32), 0)
        half_rows = wgt.rearrange("p (h c) -> (p h) c", h=2)[0 : 2 * P : GROUP + 1, :]
        nc.sync.dma_start(out=chunks[:], in_=half_rows.rearrange("m (s c) -> m s c", c=BLOCK))
        load_plane(0, 0)
        nc.sync.dma_start(lists[:], offs)
        nc.sync.dma_start(out=weight[:, TURNED:S], in_=wgt[:, TURNED:S])
        for i in range(1, PACK):
            load_plane(0, i)
        for i in range(PACK):
            load_plane(1, i)
        for q in range(4):
            nc.sync.dma_start(
                out=w_sc[32 * q : 32 * q + 4, :, :].bitcast(I32),
                in_=w_scales.bitcast(I32)[:, 4 * q : 4 * q + 4, :].rearrange("a q n -> q a n"),
            )
        nc.sync.dma_start(out=w_codes[:].bitcast(I32), in_=w_words.bitcast(I32).rearrange("a p n -> p a n"))

        def pick(a, i, m0, m1, slot):
            nc.vector.tensor_tensor(
                stage[:, slot : slot + m1 - m0, :].rearrange("p m n -> p (m n)"),
                planes[a][i][:].indirect(lists[:, P * m0 // GROUP : P * m1 // GROUP]),
                weight[:, P * m0 : P * m1],
                MULT,
            )

        def weave(copy, dst, src):
            copy(dst.rearrange("p (c n) i -> p c i n", n=RUN), src.rearrange("p i (c n) -> p c i n", n=RUN))

        def slots(first, step, count):
            return stage[:, first : first + step * (count - 1) + 1 : step, :]

        def quantise(a, c0, c1, values, scale):
            nc.vector.quantize_mx(
                out=codes[a][:, c0:c1].bitcast(E4M3X4),
                scales=scale,
                in_=values.rearrange("p n i -> p (n i)"),
            )

        def multiply(a, m, scale):
            sums = [banks[m]] if m < ONE_BANK else halves[m]
            width = N_OUT // len(sums)
            for h, acc in enumerate(sums):
                nc.tensor.matmul_mx(
                    out=acc[:],
                    lhsT=codes[a][:, P * m : P * (m + 1)].bitcast(E4M3X4),
                    lhsT_scale=scale,
                    rhs=w_codes[:, a, 2 * width * h : 2 * width * (h + 1)].bitcast(E2M1X4),
                    rhs_scale=w_sc[:, a, width * h : width * (h + 1)],
                    start=(a == 0),
                    stop=(a == PASSES - 1),
                )

        def second_pass(m):
            scale = scales[1][:, P * m : P * (m + 1)]
            quantise(1, P * m, P * (m + 1), woven1[m][:], scale)
            multiply(1, m, scale)

        def store(m):
            if m < ONE_BANK:
                nc.scalar.copy(results[m][:], banks[m][:])
            else:
                nc.vector.tensor_copy(results[m][:, 0:HALF], halves[m][0][:])
                nc.scalar.copy(results[m][:, HALF:N_OUT], halves[m][1][:])
            nc.sync.dma_start(out=out[P * m : P * (m + 1), :], in_=results[m][:])

        nc.vector.transpose(turned[:], chunks[:])
        by_chunk = turned[:].rearrange("p (h s) -> p s h", h=2)
        for c0, c1 in ((0, P), (P, TURNED)):
            nc.vector.tensor_copy(
                spread[:, c0:c1].rearrange("p (s h r) -> p s h r", h=2, r=GROUP),
                by_chunk[:, c0 // BLOCK : c1 // BLOCK, :].unsqueeze(3).to_broadcast([P, (c1 - c0) // BLOCK, 2, GROUP]),
            )
        for c0, c1 in ((0, P), (P, LAST * P), (LAST * P, LAST * P + BLOCK), (LAST * P + BLOCK, TURNED)):
            nc.vector.transpose(weight[:, c0:c1], spread[:, c0:c1])

        pick(0, 0, 0, 1, PASS0)
        pick(0, 0, 1, TILES, PASS0 + 1)
        for i in range(1, PACK):
            pick(0, i, 0, TILES, PASS0 + TILES * i)
        staged0 = stage[:, PASS0:SLOTS, :].rearrange("p (i m) n -> p i (m n)", i=PACK)

        def weave0(c0, c1):
            weave(nc.scalar.copy, woven0[:, c0:c1, :], staged0[:, :, c0:c1])

        weave0(0, 2 * P - HELD)
        weave0(2 * P, S)

        for i in range(2):
            pick(1, i, 0, TILES, EARLY + TILES * i)
        early = stage[:, EARLY : EARLY + 2 * TILES, :].rearrange("p (i m) n -> p i (m n)", i=2)
        weave(nc.scalar.copy, woven_pairs[:, 0:P, 0:2], early[:, :, P : 2 * P])
        weave0(2 * P - HELD, 2 * P)
        weave(nc.scalar.copy, woven_pairs[:, P : LAST * P, 0:2], early[:, :, 2 * P : S])
        pick(1, 2, 0, LAST, THIRD)

        parts = ((0, P // 2), (P // 2, P))

        def first_pass(m0, m1):
            quantise(0, P * m0, P * m1, woven0[:, P * m0 : P * m1, :], scales[0][:, P * m0 : P * m1])
            for m in range(m0, m1):
                multiply(0, m, scales[0][:, P * m : P * (m + 1)])

        def late(m):
            pick(1, 3, m, m + 1, PASS0 + m)
            if m == 0:
                for c0, c1 in parts:
                    weave(nc.scalar.copy, woven1[m][:, c0:c1, :], slots(EARLY, TILES, PACK)[:, :, c0:c1])
            else:
                weave(nc.scalar.copy, woven1[m][:, :, 2:4], slots(THIRD + m, PASS0 - THIRD, 2))

        first_pass(2, 3)
        late(2)
        late(0)
        first_pass(0, 2)
        late(1)

        second_pass(2)
        store(2)
        pick(1, 2, LAST, TILES, THIRD + 2)
        for c0, c1 in parts:
            quantise(1, c0, c1, woven1[0][:, c0:c1, :], scales[1][:, c0:c1])
        multiply(1, 0, scales[1][:, 0:P])
        store(0)
        pick(1, 3, LAST, TILES, PASS0)

        second_pass(1)

        for c0, c1 in parts:
            weave(nc.vector.tensor_copy, woven1[LAST][:, c0:c1, 2:4], slots(THIRD + 2, PASS0 - THIRD - 2, 2)[:, :, c0:c1])
        last_scale = keep.tile([P, P], U8, name="last_scale", tag="x13", align_bytes=256)
        quantise(0, P * LAST, S, woven0[:, P * LAST : S, :], last_scale[:])
        multiply(0, LAST, last_scale[:])
        for c0, c1 in parts:
            at = P * LAST
            quantise(1, at + c0, at + c1, woven1[LAST][:, c0:c1, :], scales[1][:, at + c0 : at + c1])
        multiply(1, LAST, scales[1][:, P * LAST : S])
        for m in (1, LAST):
            store(m)
